import numpy as np
import ml_dtypes


def mxq(x, axis, fmt="e4m3"):
    dtype, down = {"e4m3": (ml_dtypes.float8_e4m3fn, 7), "e5m2": (ml_dtypes.float8_e5m2, 14)}[fmt]
    v = np.moveaxis(np.asarray(x, np.float32).astype(ml_dtypes.bfloat16).astype(np.float64), axis, -1)
    blocks = v.reshape(v.shape[:-1] + (-1, 32))
    amax = np.abs(blocks).max(-1, keepdims=True)
    byte = np.maximum(np.where(amax > 0, np.frexp(amax)[1] - 1 + 127, 0) - down, 1)
    scale = np.exp2(byte - 127.0)
    codes = (blocks / scale).astype(np.float32).astype(dtype).astype(np.float64)
    return np.moveaxis((codes * scale).reshape(v.shape), -1, axis)


WIDE = False


def mx_kscale(k):
    if not WIDE:
        return np.ones(k)
    levels = np.array([10, -10, 5, -5, 0])
    if k % 512:
        return np.exp2(np.random.permutation(np.resize(levels, k // 32))).repeat(32)
    a = np.empty((k // 512, 16))
    for p in range(k // 512):
        a[p, :8] = np.random.permutation(np.resize(levels, 8))
        for g in range(8):
            far = levels[np.abs(levels - a[p, g]) >= 10]
            a[p, g + 8] = far[np.random.randint(len(far))]
    return np.exp2(a.ravel()).repeat(32)


def f64(x):
    return np.asarray(x).astype(np.float64)


def striped(idx):
    return np.tile(idx.reshape(-1, 16).T, (8, 1)).astype(np.uint16)


def unstriped(offs):
    return offs[:16].T.reshape(-1).astype(np.int64)


E2M1 = np.array([0.0, 0.5, 1.0, 1.5, 2.0, 3.0, 4.0, 6.0, -0.0, -0.5, -1.0, -1.5, -2.0, -3.0, -4.0, -6.0])


def pack_weight(w, fmt):
    k, n = w.shape
    w = f64(np.asarray(w, np.float32).astype(ml_dtypes.bfloat16)).reshape(k // 32, 32, n)
    amax = np.abs(w).max(1)
    if fmt == "e4m3":
        byte = np.frexp(amax)[1] - 1 + 127 - 7
    else:
        mant, ex = np.frexp(amax / 6.0)
        byte = np.where(mant > 0.5, ex, ex - 1) + 127
    byte = np.clip(np.where(amax > 0, byte, 1), 1, 254)
    scaled = (w * np.exp2(127.0 - byte)[:, None, :]).reshape(k, n).astype(np.float32)
    by_word = np.ascontiguousarray(scaled.reshape(k // 512, 128, 4, n).transpose(0, 1, 3, 2))
    if fmt == "e4m3":
        words = by_word.astype(ml_dtypes.float8_e4m3fn).view(np.uint8)
    else:
        c = by_word.astype(ml_dtypes.float4_e2m1fn).view(np.uint8) & 0xF
        words = (c[..., 0::2] | (c[..., 1::2] << 4)).reshape(k // 512, 128, 2 * n)
    return np.ascontiguousarray(words), np.ascontiguousarray(byte.astype(np.uint8).reshape(k // 512, 16, n))


def unpack_weight(words, scales, fmt):
    g, _, n = scales.shape
    words = np.ascontiguousarray(words).reshape(g, 128, n, -1)
    if fmt == "e4m3":
        vals = words.view(ml_dtypes.float8_e4m3fn).astype(np.float64)
    else:
        nib = np.empty((g, 128, n, 4), np.uint8)
        nib[..., 0::2] = words & 0xF
        nib[..., 1::2] = words >> 4
        vals = E2M1[nib]
    vals = vals * np.repeat(np.exp2(scales.astype(np.float64) - 127.0), 8, axis=1)[..., None]
    return vals.transpose(0, 1, 3, 2).reshape(g * 512, n)


def gelu(v):
    return 0.5 * v * (1.0 + np.tanh(np.sqrt(2.0 / np.pi) * (v + 0.044715 * v**3)))


def striped8(idx):
    return np.concatenate([v.reshape(-1, 16).T for v in idx]).astype(np.uint16)


def unstriped8(offs):
    return np.stack([offs[16 * g:16 * g + 16].T.reshape(-1) for g in range(8)]).astype(np.int64)


def heads(h, wgt, idx8):
    r = np.arange(h.shape[0])
    return wgt[r // 4 % 128] * h[r[:, None], idx8[r % 512 // 64]]


def bf(x):
    return np.asarray(x, np.float32).astype(ml_dtypes.bfloat16)


def planes(Y):
    n, m = Y.shape
    b = f64(bf(Y)).reshape(n // 32, 32, m)
    amax = np.abs(b).max(1)
    byte = np.clip(np.where(amax > 0, np.frexp(amax)[1] - 1 + 127 - 7, 1), 1, 254)
    codes = (b * np.exp2(127.0 - byte)[:, None, :]).reshape(n, m).astype(np.float32).astype(ml_dtypes.float8_e4m3fn).view(np.uint8)
    words = codes.reshape(n // 512, 128, 4, m).transpose(0, 1, 3, 2)
    return np.ascontiguousarray(words), np.ascontiguousarray(byte.astype(np.uint8).reshape(n // 512, 16, m))


K, T, S, P, H, N = 1024, 2048, 1024, 512, 1024, 1024

def setup_inputs():
    n = np.random.standard_normal
    s = mx_kscale(K)[:, None]
    u = mx_kscale(H)[:, None]
    tab_words, tab_scales = pack_weight(n((K, T)) * s, "e4m3")
    w4_words, w4_scales = pack_weight(n((K, H)) / np.sqrt(K) / s * u.T, "e2m1")
    offs = striped(np.random.permutation(T)[:S])
    offs2 = striped8(np.stack([np.random.permutation(S)[:P] for _ in range(8)]))
    wgt = np.repeat(np.random.uniform(0.5, 2.0, (8, P)), 16, axis=0)
    return {
        "tab_words": tab_words, "tab_scales": tab_scales,
        "offs": offs, "offs2": offs2,
        "wgt": wgt.astype(np.float32),
        "w4_words": w4_words, "w4_scales": w4_scales,
        "mic": (n((H, P)) * u).astype(np.float32),
        "power": np.random.uniform(0.5, 2.0, (H, P)).astype(np.float32),
        "cor": (n((H, N)) / np.sqrt(H) / u).astype(np.float32),
        "prev": n((N, P)).astype(np.float32),
        "gain": np.exp(0.8 * n(N)).astype(np.float32),
    }

def reference(tab_words, tab_scales, offs, offs2, wgt, w4_words, w4_scales, mic, power, cor, prev, gain):
    v = unpack_weight(tab_words, tab_scales, "e4m3")[:, unstriped(offs)]
    w4 = unpack_weight(w4_words, w4_scales, "e2m1")
    h = w4.T @ v
    x = heads(h, f64(wgt), unstriped8(offs2))
    res = f64(mic) - x
    z = res * (1.0 / f64(power))
    step = mxq(f64(cor), 0, "e4m3").T @ mxq(z, 0, "e4m3")
    y = f64(gain)[:, None] * (f64(prev) + step)
    words, scales = planes(y)
    return y, words, scales

@@ -1,0 +1,213 @@
+from contextlib import ExitStack
+
+import concourse.mybir as mybir
+
+K, T, S, M, H, N = 1024, 2048, 1024, 512, 1024, 1024
+FLOPS = 2 * K * H * S + 2 * H * N * M
+
+F32 = mybir.dt.float32
+BF16 = mybir.dt.bfloat16
+I32 = mybir.dt.int32
+U32 = mybir.dt.uint32
+U16 = mybir.dt.uint16
+U8 = mybir.dt.uint8
+FP8X4 = mybir.dt.float8_e4m3fn_x4
+FP4X4 = mybir.dt.float4_e2m1fn_x4
+ACT = mybir.ActivationFunctionType
+ALU = mybir.AluOpType
+
+P = 128
+BANK = 512
+
+
+def tile_list_subband_echo_update_kernel(
+    tc, tab_words, tab_scales, offs, offs2, wgt, w4_words, w4_scales, mic, power, cor, prev, gain, out_0, out_1, out_2
+):
+    nc = tc.nc
+    with ExitStack() as ctx:
+        lists = ctx.enter_context(tc.tile_pool(name="lists", bufs=1))
+        sb = ctx.enter_context(tc.tile_pool(name="sb", bufs=1))
+        psum = ctx.enter_context(tc.psum_pool(name="psum", bufs=1))
+
+        def tile(shape, dtype, name):
+            return sb.tile(shape, dtype, name=name, align_bytes=64)
+
+        tab_sc = tile([P, 2, T], U8, "tab_sc")
+        nc.vector.memset(tab_sc[:].bitcast(I32), 0)
+        w4_sc = tile([P, 2, H], U8, "w4_sc")
+        nc.gpsimd.memset(w4_sc[:].bitcast(I32), 0)
+        one = tile([P, 1], F32, "one")
+        nc.vector.memset(one[:], 1.0)
+
+        w4_raw = tile([P, 2, H // 2], I32, "w4_raw")
+        nc.sync.dma_start(out=w4_raw[:], in_=w4_words.bitcast(I32).rearrange("a p c -> p a c"))
+        for q in range(4):
+            nc.sync.dma_start(
+                out=tab_sc[32 * q : 32 * q + 4, :, :].bitcast(I32),
+                in_=tab_scales[:, 4 * q : 4 * q + 4, :].bitcast(I32).rearrange("a r c -> r a c"),
+            )
+        idx = lists.tile([P, S // 16], U16, name="idx")
+        nc.sync.dma_start(idx[:], offs)
+        tab = []
+        for a in range(2):
+            words = tile([P, T], I32, f"tab{a}")
+            nc.sync.dma_start(out=words[:], in_=tab_words[a].rearrange("p t i -> p (t i)").bitcast(I32))
+            tab.append(words)
+        for q in range(4):
+            nc.scalar.dma_start(
+                out=w4_sc[32 * q : 32 * q + 4, :, :].bitcast(I32),
+                in_=w4_scales[:, 4 * q : 4 * q + 4, :].bitcast(I32).rearrange("a r c -> r a c"),
+            )
+        warm = tile([P, 1], F32, "warm")
+        nc.scalar.activation(out=warm[:], in_=one[:], func=ACT.Abs_reciprocal_sqrt)
+
+        def load_rows(src, b, name):
+            rows = tile([P, 4, M], F32, name)
+            nc.sync.dma_start(out=rows[:], in_=src[512 * b : 512 * (b + 1), :].rearrange("(p i) m -> p i m", i=4))
+            return rows
+
+        power_sb = [load_rows(power, 0, "power0")]
+        idx2 = lists.tile([P, M // 16], U16, name="idx2")
+        nc.sync.dma_start(idx2[:], offs2)
+        wgt_sb = tile([P, M], F32, "wgt_sb")
+        nc.sync.dma_start(out=wgt_sb[:], in_=wgt)
+        mic_sb = [load_rows(mic, 0, "mic0")]
+        power_sb.append(load_rows(power, 1, "power1"))
+        mic_sb.append(load_rows(mic, 1, "mic1"))
+        cor_raw = {}
+        for g in range(2):
+            for b in range(2):
+                cor_raw[b, g] = load_rows(cor[:, 512 * g : 512 * (g + 1)], b, f"cor{b}{g}")
+        gain_sb = tile([P, 2, 4], F32, "gain_sb")
+        nc.sync.dma_start(out=gain_sb[:], in_=gain.rearrange("(g p t) -> p g t", g=2, t=4))
+        prev_sb = [load_rows(prev, g, f"prev{g}") for g in range(2)]
+
+        v_sc = [tile([P, S], U8, f"v_sc{a}") for a in range(2)]
+        for a in range(2):
+            nc.vector.tensor_copy(v_sc[a][:], tab_sc[:, a, :].indirect(idx[:]))
+
+        w4_dealt, w4_sc_dealt = [], []
+
+        def deal_w4(b):
+            words = tile([P, 2, 4, 2 * P], U8, f"w4_dealt{b}")
+            nc.vector.tensor_copy(
+                out=words[:].bitcast(U16),
+                in_=w4_raw[:].bitcast(U16)[:, :, 512 * b : 512 * (b + 1)].rearrange("p a (c i) -> p a i c", i=4),
+            )
+            scales = tile([P, 2, 4, P], U8, f"w4_sc_dealt{b}")
+            nc.vector.tensor_copy(
+                out=scales[:], in_=w4_sc[:, :, 512 * b : 512 * (b + 1)].rearrange("p a (c i) -> p a i c", i=4)
+            )
+            w4_dealt.append(words)
+            w4_sc_dealt.append(scales)
+
+        deal_w4(0)
+        v = [tile([P, S], U32, f"v{a}") for a in range(2)]
+        nc.vector.tensor_copy(v[0][:], tab[0][:].bitcast(U32).indirect(idx[:]))
+        for half in range(2):
+            nc.vector.tensor_copy(
+                v[1][:, BANK * half : BANK * (half + 1)],
+                tab[1][:].bitcast(U32).indirect(idx[:, 32 * half : 32 * (half + 1)]),
+            )
+        deal_w4(1)
+
+        h = {}
+        for b in range(2):
+            for i in range(4):
+                rows = tile([P, S], F32, f"h{b}{i}")
+                for half in range(2):
+                    cols = slice(BANK * half, BANK * (half + 1))
+                    acc = psum.tile([P, BANK], F32, name="acc", tag=f"bank{2 * i + half}")
+                    for a in range(2):
+                        nc.tensor.matmul_mx(
+                            out=acc[:],
+                            lhsT=w4_dealt[b][:, a, i, :].bitcast(FP4X4),
+                            lhsT_scale=w4_sc_dealt[b][:, a, i, :],
+                            rhs=v[a][:, cols].bitcast(FP8X4),
+                            rhs_scale=v_sc[a][:, cols],
+                            start=(a == 0),
+                            stop=(a == 1),
+                        )
+                    nc.scalar.copy(out=rows[:, cols], in_=acc[:])
+                h[b, i] = rows
+
+        for b in range(2):
+            for pair in range(2):
+                part = power_sb[b][:, 2 * pair : 2 * pair + 2, :]
+                nc.scalar.activation(out=part, in_=part, func=ACT.Abs_reciprocal_sqrt)
+                nc.scalar.activation(out=part, in_=part, func=ACT.Square)
+
+        z_codes, z_sc = [], []
+        for b in range(2):
+            x = tile([P, 4, M], F32, f"x{b}")
+            for i in range(4):
+                nc.vector.tensor_tensor(x[:, i, :], h[b, i][:].indirect(idx2[:]), wgt_sb[:], ALU.mult)
+            nc.vector.tensor_tensor(x[:], mic_sb[b][:], x[:], ALU.subtract)
+            z = tile([P, M, 4], BF16, f"z{b}")
+            nc.vector.tensor_tensor(
+                z[:].rearrange("p (c e) i -> p c i e", e=4),
+                x[:].rearrange("p i (c e) -> p c i e", e=4),
+                power_sb[b][:].rearrange("p i (c e) -> p c i e", e=4),
+                ALU.mult,
+            )
+            codes = tile([P, M], U32, f"z_codes{b}")
+            scales = tile([P, M], U8, f"z_sc{b}")
+            nc.vector.quantize_mx(
+                out=codes[:].bitcast(FP8X4), scales=scales[:], in_=z[:].rearrange("p m i -> p (m i)")
+            )
+            z_codes.append(codes)
+            z_sc.append(scales)
+
+        cor_codes, cor_sc = {}, {}
+        for g in range(2):
+            for b in range(2):
+                dealt = tile([P, 4, P, 4], BF16, f"cor_bf{b}{g}")
+                nc.scalar.copy(
+                    out=dealt[:].rearrange("p t c j -> p c j t"),
+                    in_=cor_raw[b, g][:].rearrange("p j (c t) -> p c j t", t=4),
+                )
+                codes = tile([P, BANK], U32, f"cor_codes{b}{g}")
+                scales = tile([P, BANK], U8, f"cor_sc{b}{g}")
+                nc.vector.quantize_mx(
+                    out=codes[:].bitcast(FP8X4), scales=scales[:], in_=dealt[:].rearrange("p t c j -> p (t c j)")
+                )
+                cor_codes[b, g], cor_sc[b, g] = codes, scales
+
+        y_sc = tile([P, 2, M], U8, "y_sc")
+        for g in range(2):
+            y = prev_sb[g]
+            for t in range(4):
+                acc = psum.tile([P, BANK], F32, name="acc", tag=f"bank{4 * g + t}")
+                cols = slice(P * t, P * (t + 1))
+                for b in range(2):
+                    nc.tensor.matmul_mx(
+                        out=acc[:],
+                        lhsT=cor_codes[b, g][:, cols].bitcast(FP8X4),
+                        lhsT_scale=cor_sc[b, g][:, cols],
+                        rhs=z_codes[b][:].bitcast(FP8X4),
+                        rhs_scale=z_sc[b][:],
+                        start=(b == 0),
+                        stop=(b == 1),
+                    )
+                nc.vector.tensor_tensor(y[:, t, :], acc[:], y[:, t, :], ALU.add)
+                nc.scalar.activation(out=y[:, t, :], in_=y[:, t, :], func=ACT.Copy, scale=gain_sb[:, g, t : t + 1])
+            rows = out_0[512 * g : 512 * (g + 1), :].rearrange("(p t) m -> p t m", t=4)
+            for pair in range(2):
+                nc.sync.dma_start(out=rows[:, 2 * pair : 2 * pair + 2, :], in_=y[:, 2 * pair : 2 * pair + 2, :])
+        for g in range(2):
+            y_bf = tile([P, M, 4], BF16, f"y_bf{g}")
+            nc.vector.tensor_copy(
+                out=y_bf[:].rearrange("p (c e) t -> p c t e", e=4),
+                in_=prev_sb[g][:].rearrange("p t (c e) -> p c t e", e=4),
+            )
+            codes = tile([P, M], I32, f"y_codes{g}")
+            nc.vector.quantize_mx(
+                out=codes[:].bitcast(FP8X4), scales=y_sc[:, g, :], in_=y_bf[:].rearrange("p m t -> p (m t)")
+            )
+            nc.sync.dma_start(out=out_1[g].rearrange("p m t -> p (m t)").bitcast(I32), in_=codes[:])
+        for q in range(4):
+            queue = nc.scalar if q % 2 else nc.sync
+            queue.dma_start(
+                out=out_2[:, 4 * q : 4 * q + 4, :].bitcast(I32).rearrange("g r m -> r g m"),
+                in_=y_sc[32 * q : 32 * q + 4, :, :].bitcast(I32),
+            )

@@ -29,13 +29,16 @@ def tile_list_subband_echo_update_kernel(
         sb = ctx.enter_context(tc.tile_pool(name="sb", bufs=1))
         psum = ctx.enter_context(tc.psum_pool(name="psum", bufs=1))
 
-        def tile(shape, dtype, name):
-            return sb.tile(shape, dtype, name=name, align_bytes=64)
+        def tile(shape, dtype, name, after=None):
+            return sb.tile(shape, dtype, name=name, tag=after or name, align_bytes=64)
 
-        tab_sc = tile([P, 2, T], U8, "tab_sc")
-        nc.vector.memset(tab_sc[:].bitcast(I32), 0)
+
+        tab_sc = tile([P, T], U8, "tab_sc")
+        nc.gpsimd.memset(tab_sc[:].bitcast(I32), 0)
         w4_sc = tile([P, 2, H], U8, "w4_sc")
-        nc.gpsimd.memset(w4_sc[:].bitcast(I32), 0)
+        nc.vector.memset(w4_sc[:].bitcast(I32), 0)
+        v_sc = [tile([P, S], U8, f"v_sc{a}") for a in range(2)]
+        nc.vector.memset(v_sc[1][:].bitcast(I32), 0)
         one = tile([P, 1], F32, "one")
         nc.vector.memset(one[:], 1.0)
 
@@ -43,30 +46,35 @@ def tile_list_subband_echo_update_kernel(
         nc.sync.dma_start(out=w4_raw[:], in_=w4_words.bitcast(I32).rearrange("a p c -> p a c"))
         for q in range(4):
             nc.sync.dma_start(
-                out=tab_sc[32 * q : 32 * q + 4, :, :].bitcast(I32),
-                in_=tab_scales[:, 4 * q : 4 * q + 4, :].bitcast(I32).rearrange("a r c -> r a c"),
+                out=tab_sc[32 * q : 32 * q + 8, :].bitcast(I32), in_=tab_scales[:, 4 * q : 4 * q + 4, :].bitcast(I32)
             )
         idx = lists.tile([P, S // 16], U16, name="idx")
         nc.sync.dma_start(idx[:], offs)
-        tab = []
-        for a in range(2):
-            words = tile([P, T], I32, f"tab{a}")
-            nc.sync.dma_start(out=words[:], in_=tab_words[a].rearrange("p t i -> p (t i)").bitcast(I32))
-            tab.append(words)
-        for q in range(4):
-            nc.scalar.dma_start(
-                out=w4_sc[32 * q : 32 * q + 4, :, :].bitcast(I32),
-                in_=w4_scales[:, 4 * q : 4 * q + 4, :].bitcast(I32).rearrange("a r c -> r a c"),
-            )
         warm = tile([P, 1], F32, "warm")
         nc.scalar.activation(out=warm[:], in_=one[:], func=ACT.Abs_reciprocal_sqrt)
 
+        def rows_of(src, b):
+            return src[512 * b : 512 * (b + 1), :].rearrange("(p i) m -> p i m", i=4)
+
         def load_rows(src, b, name):
             rows = tile([P, 4, M], F32, name)
-            nc.sync.dma_start(out=rows[:], in_=src[512 * b : 512 * (b + 1), :].rearrange("(p i) m -> p i m", i=4))
+            nc.sync.dma_start(out=rows[:], in_=rows_of(src, b))
             return rows
 
-        power_sb = [load_rows(power, 0, "power0")]
+        tab = [tile([P, T], I32, f"tab{a}") for a in range(2)]
+        power_sb = [tile([P, 4, M], F32, "power0")]
+
+        def load_pass(a):
+            nc.sync.dma_start(out=tab[a][:], in_=tab_words[a].rearrange("p t i -> p (t i)").bitcast(I32))
+            nc.sync.dma_start(out=power_sb[0][:, 2 * a : 2 * a + 2, :], in_=rows_of(power, 0)[:, 2 * a : 2 * a + 2, :])
+
+        load_pass(0)
+        for q in range(4):
+            nc.sync.dma_start(
+                out=w4_sc[32 * q : 32 * q + 4, :, :].bitcast(I32),
+                in_=w4_scales[:, 4 * q : 4 * q + 4, :].bitcast(I32).rearrange("a r c -> r a c"),
+            )
+        load_pass(1)
         idx2 = lists.tile([P, M // 16], U16, name="idx2")
         nc.sync.dma_start(idx2[:], offs2)
         wgt_sb = tile([P, M], F32, "wgt_sb")
@@ -82,19 +90,18 @@ def tile_list_subband_echo_update_kernel(
         nc.sync.dma_start(out=gain_sb[:], in_=gain.rearrange("(g p t) -> p g t", g=2, t=4))
         prev_sb = [load_rows(prev, g, f"prev{g}") for g in range(2)]
 
-        v_sc = [tile([P, S], U8, f"v_sc{a}") for a in range(2)]
-        for a in range(2):
-            nc.vector.tensor_copy(v_sc[a][:], tab_sc[:, a, :].indirect(idx[:]))
+        nc.vector.tensor_copy(v_sc[0][:], tab_sc[:].indirect(idx[:]))
+        nc.scalar.dma_start(out=v_sc[1][0:112, :].bitcast(I32), in_=v_sc[0][4:116, :].bitcast(I32))
 
         w4_dealt, w4_sc_dealt = [], []
 
-        def deal_w4(b):
-            words = tile([P, 2, 4, 2 * P], U8, f"w4_dealt{b}")
+        def deal_w4(b, words_after=None, scales_after=None):
+            words = tile([P, 2, 4, 2 * P], U8, f"w4_dealt{b}", words_after)
             nc.vector.tensor_copy(
                 out=words[:].bitcast(U16),
                 in_=w4_raw[:].bitcast(U16)[:, :, 512 * b : 512 * (b + 1)].rearrange("p a (c i) -> p a i c", i=4),
             )
-            scales = tile([P, 2, 4, P], U8, f"w4_sc_dealt{b}")
+            scales = tile([P, 2, 4, P], U8, f"w4_sc_dealt{b}", scales_after)
             nc.vector.tensor_copy(
                 out=scales[:], in_=w4_sc[:, :, 512 * b : 512 * (b + 1)].rearrange("p a (c i) -> p a i c", i=4)
             )
@@ -109,100 +116,144 @@ def tile_list_subband_echo_update_kernel(
                 v[1][:, BANK * half : BANK * (half + 1)],
                 tab[1][:].bitcast(U32).indirect(idx[:, 32 * half : 32 * (half + 1)]),
             )
-        deal_w4(1)
+        deal_w4(1, "tab1", "w4_raw")
+
+        def on_power(func, b, pair):
+            part = power_sb[b][:, 2 * pair : 2 * pair + 2, :]
+            nc.scalar.activation(out=part, in_=part, func=func)
 
         h = {}
-        for b in range(2):
-            for i in range(4):
-                rows = tile([P, S], F32, f"h{b}{i}")
-                for half in range(2):
-                    cols = slice(BANK * half, BANK * (half + 1))
-                    acc = psum.tile([P, BANK], F32, name="acc", tag=f"bank{2 * i + half}")
-                    for a in range(2):
-                        nc.tensor.matmul_mx(
-                            out=acc[:],
-                            lhsT=w4_dealt[b][:, a, i, :].bitcast(FP4X4),
-                            lhsT_scale=w4_sc_dealt[b][:, a, i, :],
-                            rhs=v[a][:, cols].bitcast(FP8X4),
-                            rhs_scale=v_sc[a][:, cols],
-                            start=(a == 0),
-                            stop=(a == 1),
-                        )
-                    nc.scalar.copy(out=rows[:, cols], in_=acc[:])
-                h[b, i] = rows
 
-        for b in range(2):
-            for pair in range(2):
-                part = power_sb[b][:, 2 * pair : 2 * pair + 2, :]
-                nc.scalar.activation(out=part, in_=part, func=ACT.Abs_reciprocal_sqrt)
-                nc.scalar.activation(out=part, in_=part, func=ACT.Square)
-
-        z_codes, z_sc = [], []
-        for b in range(2):
-            x = tile([P, 4, M], F32, f"x{b}")
-            for i in range(4):
-                nc.vector.tensor_tensor(x[:, i, :], h[b, i][:].indirect(idx2[:]), wgt_sb[:], ALU.mult)
-            nc.vector.tensor_tensor(x[:], mic_sb[b][:], x[:], ALU.subtract)
-            z = tile([P, M, 4], BF16, f"z{b}")
-            nc.vector.tensor_tensor(
-                z[:].rearrange("p (c e) i -> p c i e", e=4),
-                x[:].rearrange("p i (c e) -> p c i e", e=4),
-                power_sb[b][:].rearrange("p i (c e) -> p c i e", e=4),
-                ALU.mult,
-            )
-            codes = tile([P, M], U32, f"z_codes{b}")
-            scales = tile([P, M], U8, f"z_sc{b}")
-            nc.vector.quantize_mx(
-                out=codes[:].bitcast(FP8X4), scales=scales[:], in_=z[:].rearrange("p m i -> p (m i)")
-            )
-            z_codes.append(codes)
-            z_sc.append(scales)
-
-        cor_codes, cor_sc = {}, {}
-        for g in range(2):
-            for b in range(2):
-                dealt = tile([P, 4, P, 4], BF16, f"cor_bf{b}{g}")
-                nc.scalar.copy(
-                    out=dealt[:].rearrange("p t c j -> p c j t"),
-                    in_=cor_raw[b, g][:].rearrange("p j (c t) -> p c j t", t=4),
-                )
-                codes = tile([P, BANK], U32, f"cor_codes{b}{g}")
-                scales = tile([P, BANK], U8, f"cor_sc{b}{g}")
-                nc.vector.quantize_mx(
-                    out=codes[:].bitcast(FP8X4), scales=scales[:], in_=dealt[:].rearrange("p t c j -> p (t c j)")
-                )
-                cor_codes[b, g], cor_sc[b, g] = codes, scales
-
-        y_sc = tile([P, 2, M], U8, "y_sc")
-        for g in range(2):
-            y = prev_sb[g]
-            for t in range(4):
-                acc = psum.tile([P, BANK], F32, name="acc", tag=f"bank{4 * g + t}")
-                cols = slice(P * t, P * (t + 1))
-                for b in range(2):
+        def filter_rows(b, i):
+            rows = tile([P, S], F32, f"h{b}{i}")
+            for half in range(2):
+                cols = slice(BANK * half, BANK * (half + 1))
+                acc = psum.tile([P, BANK], F32, name="acc", tag=f"bank{2 * i + half}")
+                for a in range(2):
                     nc.tensor.matmul_mx(
                         out=acc[:],
-                        lhsT=cor_codes[b, g][:, cols].bitcast(FP8X4),
-                        lhsT_scale=cor_sc[b, g][:, cols],
-                        rhs=z_codes[b][:].bitcast(FP8X4),
-                        rhs_scale=z_sc[b][:],
-                        start=(b == 0),
-                        stop=(b == 1),
+                        lhsT=w4_dealt[b][:, a, i, :].bitcast(FP4X4),
+                        lhsT_scale=w4_sc_dealt[b][:, a, i, :],
+                        rhs=v[a][:, cols].bitcast(FP8X4),
+                        rhs_scale=v_sc[a][:, cols],
+                        start=(a == 0),
+                        stop=(a == 1),
                     )
-                nc.vector.tensor_tensor(y[:, t, :], acc[:], y[:, t, :], ALU.add)
-                nc.scalar.activation(out=y[:, t, :], in_=y[:, t, :], func=ACT.Copy, scale=gain_sb[:, g, t : t + 1])
-            rows = out_0[512 * g : 512 * (g + 1), :].rearrange("(p t) m -> p t m", t=4)
-            for pair in range(2):
-                nc.sync.dma_start(out=rows[:, 2 * pair : 2 * pair + 2, :], in_=y[:, 2 * pair : 2 * pair + 2, :])
-        for g in range(2):
-            y_bf = tile([P, M, 4], BF16, f"y_bf{g}")
-            nc.vector.tensor_copy(
-                out=y_bf[:].rearrange("p (c e) t -> p c t e", e=4),
-                in_=prev_sb[g][:].rearrange("p t (c e) -> p c t e", e=4),
+                nc.scalar.copy(out=rows[:, cols], in_=acc[:])
+            h[b, i] = rows
+
+        x = {}
+
+        def pick(b, i):
+            if i == 0:
+                x[b] = tile([P, 4, M], F32, f"x{b}")
+            nc.vector.tensor_tensor(x[b][:, i, :], h[b, i][:].indirect(idx2[:]), wgt_sb[:], ALU.mult)
+
+        z, z_codes, z_sc = {}, {}, {}
+
+        def residual(b):
+            nc.vector.tensor_tensor(x[b][:], mic_sb[b][:], x[b][:], ALU.subtract)
+            z[b] = tile([P, M, 4], BF16, f"z{b}")
+            nc.vector.tensor_tensor(
+                z[b][:].rearrange("p (c e) i -> p c i e", e=2),
+                x[b][:].rearrange("p i (c e) -> p c i e", e=2),
+                power_sb[b][:].rearrange("p i (c e) -> p c i e", e=2),
+                ALU.mult,
             )
+
+        def quantize_z(b, after=None):
+            z_codes[b] = tile([P, M], U32, f"z_codes{b}", after)
+            z_sc[b] = tile([P, M], U8, f"z_sc{b}")
+            nc.vector.quantize_mx(
+                out=z_codes[b][:].bitcast(FP8X4), scales=z_sc[b][:], in_=z[b][:].rearrange("p m i -> p (m i)")
+            )
+
+        cor_codes, cor_sc = {}, {}
+
+        def quantize_cor(b, g):
+            dealt = tile([P, 4, P, 4], BF16, f"cor_bf{b}{g}")
+            nc.scalar.copy(
+                out=dealt[:].rearrange("p t c j -> p c j t"),
+                in_=cor_raw[b, g][:].rearrange("p j (c t) -> p c j t", t=4),
+            )
+            codes = tile([P, BANK], U32, f"cor_codes{b}{g}")
+            scales = tile([P, BANK], U8, f"cor_sc{b}{g}")
+            nc.vector.quantize_mx(
+                out=codes[:].bitcast(FP8X4), scales=scales[:], in_=dealt[:].rearrange("p t c j -> p (t c j)")
+            )
+            cor_codes[b, g], cor_sc[b, g] = codes, scales
+
+        on_power(ACT.Abs_reciprocal_sqrt, 0, 0)
+        on_power(ACT.Square, 0, 0)
+        on_power(ACT.Abs_reciprocal_sqrt, 0, 1)
+        for i in range(4):
+            filter_rows(0, i)
+        on_power(ACT.Square, 0, 1)
+        for i in range(4):
+            filter_rows(1, i)
+        for pair in range(2):
+            on_power(ACT.Abs_reciprocal_sqrt, 1, pair)
+            on_power(ACT.Square, 1, pair)
+        for i in range(4):
+            pick(0, i)
+        residual(0)
+        for i in range(4):
+            pick(1, i)
+        quantize_z(0)
+        residual(1)
+        quantize_cor(0, 0)
+        quantize_cor(1, 0)
+        quantize_z(1, "cor_bf10")
+        quantize_cor(0, 1)
+        quantize_cor(1, 1)
+
+        def step(g, t):
+            acc = psum.tile([P, BANK], F32, name="acc", tag=f"bank{4 * g + t}")
+            cols = slice(P * t, P * (t + 1))
+            for b in range(2):
+                nc.tensor.matmul_mx(
+                    out=acc[:],
+                    lhsT=cor_codes[b, g][:, cols].bitcast(FP8X4),
+                    lhsT_scale=cor_sc[b, g][:, cols],
+                    rhs=z_codes[b][:].bitcast(FP8X4),
+                    rhs_scale=z_sc[b][:],
+                    start=(b == 0),
+                    stop=(b == 1),
+                )
+            return acc
+
+        def store_y(g, y, t0, t1):
+            rows = out_0[512 * g : 512 * (g + 1), :].rearrange("(p t) m -> p t m", t=4)
+            nc.sync.dma_start(out=rows[:, t0:t1, :], in_=y[:, t0:t1, :])
+
+        y0 = prev_sb[0]
+        for t in range(4):
+            acc = step(0, t)
+            nc.vector.tensor_tensor(y0[:, t, :], acc[:], y0[:, t, :], ALU.add)
+            nc.scalar.activation(out=y0[:, t, :], in_=y0[:, t, :], func=ACT.Copy, scale=gain_sb[:, 0, t : t + 1])
+            if t % 2:
+                store_y(0, y0, t - 1, t + 1)
+        y1 = tile([P, 4, M], F32, "y1", "cor_bf11")
+        for t in range(4):
+            nc.gpsimd.tensor_scalar(y1[:, t, :], prev_sb[1][:, t, :], gain_sb[:, 1, t : t + 1], 0.0, ALU.mult, ALU.add)
+        for t in range(4):
+            acc = step(1, t)
+            nc.vector.scalar_tensor_tensor(y1[:, t, :], acc[:], gain_sb[:, 1, t : t + 1], y1[:, t, :], ALU.mult, ALU.add)
+            if t % 2:
+                store_y(1, y1, t - 1, t + 1)
+
+        y_sc = tile([P, 2, M], U8, "y_sc")
+        y_bf = [tile([P, M, 4], BF16, f"y_bf{g}") for g in range(2)]
+        nc.scalar.copy(
+            out=y_bf[0][:].rearrange("p (c e) t -> p c t e", e=2), in_=y0[:].rearrange("p t (c e) -> p c t e", e=2)
+        )
+        nc.vector.tensor_copy(
+            out=y_bf[1][:].rearrange("p (c e) t -> p c t e", e=2), in_=y1[:].rearrange("p t (c e) -> p c t e", e=2)
+        )
+        for g in range(2):
             codes = tile([P, M], I32, f"y_codes{g}")
             nc.vector.quantize_mx(
-                out=codes[:].bitcast(FP8X4), scales=y_sc[:, g, :], in_=y_bf[:].rearrange("p m t -> p (m t)")
+                out=codes[:].bitcast(FP8X4), scales=y_sc[:, g, :], in_=y_bf[g][:].rearrange("p m t -> p (m t)")
             )
             nc.sync.dma_start(out=out_1[g].rearrange("p m t -> p (m t)").bitcast(I32), in_=codes[:])
         for q in range(4):

@@ -17,7 +17,11 @@ ACT = mybir.ActivationFunctionType
 ALU = mybir.AluOpType
 
 P = 128
+PACK = 4
+PASS = P * PACK
 BANK = 512
+H_BANKS = 3
+SCALAR_COLS = 192
 
 
 def tile_list_subband_echo_update_kernel(
@@ -26,12 +30,22 @@ def tile_list_subband_echo_update_kernel(
     nc = tc.nc
     with ExitStack() as ctx:
         lists = ctx.enter_context(tc.tile_pool(name="lists", bufs=1))
-        sb = ctx.enter_context(tc.tile_pool(name="sb", bufs=1))
+        sbuf = ctx.enter_context(tc.tile_pool(name="sbuf", bufs=1))
         psum = ctx.enter_context(tc.psum_pool(name="psum", bufs=1))
 
-        def tile(shape, dtype, name, after=None):
-            return sb.tile(shape, dtype, name=name, tag=after or name, align_bytes=64)
+        def tile(shape, dtype, name, on=None):
+            return sbuf.tile(shape, dtype, name=name, tag=on or name, align_bytes=64)
 
+        def group_rows(src, b):
+            return src[PASS * b : PASS * (b + 1), :].rearrange("(p i) m -> p i m", i=PACK)
+
+        def load_group(src, b, name):
+            rows = tile([P, PACK, M], F32, name)
+            nc.sync.dma_start(out=rows[:], in_=group_rows(src, b))
+            return rows
+
+        def pair_of(rows, pair):
+            return rows[:, 2 * pair : 2 * pair + 2, :]
 
         tab_sc = tile([P, T], U8, "tab_sc")
         nc.gpsimd.memset(tab_sc[:].bitcast(I32), 0)
@@ -41,6 +55,8 @@ def tile_list_subband_echo_update_kernel(
         nc.vector.memset(v_sc[1][:].bitcast(I32), 0)
         one = tile([P, 1], F32, "one")
         nc.vector.memset(one[:], 1.0)
+        warm = tile([P, 1], F32, "warm")
+        nc.scalar.activation(out=warm[:], in_=one[:], func=ACT.Abs_reciprocal_sqrt)
 
         w4_raw = tile([P, 2, H // 2], I32, "w4_raw")
         nc.sync.dma_start(out=w4_raw[:], in_=w4_words.bitcast(I32).rearrange("a p c -> p a c"))
@@ -50,206 +66,200 @@ def tile_list_subband_echo_update_kernel(
             )
         idx = lists.tile([P, S // 16], U16, name="idx")
         nc.sync.dma_start(idx[:], offs)
-        warm = tile([P, 1], F32, "warm")
-        nc.scalar.activation(out=warm[:], in_=one[:], func=ACT.Abs_reciprocal_sqrt)
 
-        def rows_of(src, b):
-            return src[512 * b : 512 * (b + 1), :].rearrange("(p i) m -> p i m", i=4)
+        def load_table(a):
+            words = tile([P, T], I32, f"tab{a}")
+            nc.sync.dma_start(out=words[:], in_=tab_words[a].rearrange("p t i -> p (t i)").bitcast(I32))
+            return words
 
-        def load_rows(src, b, name):
-            rows = tile([P, 4, M], F32, name)
-            nc.sync.dma_start(out=rows[:], in_=rows_of(src, b))
-            return rows
-
-        tab = [tile([P, T], I32, f"tab{a}") for a in range(2)]
-        power_sb = [tile([P, 4, M], F32, "power0")]
-
-        def load_pass(a):
-            nc.sync.dma_start(out=tab[a][:], in_=tab_words[a].rearrange("p t i -> p (t i)").bitcast(I32))
-            nc.sync.dma_start(out=power_sb[0][:, 2 * a : 2 * a + 2, :], in_=rows_of(power, 0)[:, 2 * a : 2 * a + 2, :])
-
-        load_pass(0)
+        tab = [load_table(0)]
+        power0 = tile([P, PACK, M], F32, "power0")
+        nc.sync.dma_start(out=pair_of(power0, 0), in_=pair_of(group_rows(power, 0), 0))
         for q in range(4):
             nc.sync.dma_start(
                 out=w4_sc[32 * q : 32 * q + 4, :, :].bitcast(I32),
                 in_=w4_scales[:, 4 * q : 4 * q + 4, :].bitcast(I32).rearrange("a r c -> r a c"),
             )
-        load_pass(1)
+        tab.append(load_table(1))
+        power1_early = [tile([P, M], F32, f"power1_early{i}", f"h0{i}") for i in range(2)]
+        for i in range(2):
+            nc.sync.dma_start(out=power1_early[i][:], in_=group_rows(power, 1)[:, i, :])
         idx2 = lists.tile([P, M // 16], U16, name="idx2")
         nc.sync.dma_start(idx2[:], offs2)
         wgt_sb = tile([P, M], F32, "wgt_sb")
         nc.sync.dma_start(out=wgt_sb[:], in_=wgt)
-        mic_sb = [load_rows(mic, 0, "mic0")]
-        power_sb.append(load_rows(power, 1, "power1"))
-        mic_sb.append(load_rows(mic, 1, "mic1"))
-        cor_raw = {}
+        nc.sync.dma_start(out=pair_of(power0, 1), in_=pair_of(group_rows(power, 0), 1))
+        mic_sb = [load_group(mic, 0, "mic0")]
+        cor_raw = {(0, g): load_group(cor[:, PASS * g : PASS * (g + 1)], 0, f"cor0{g}") for g in range(2)}
+        mic_sb.append(load_group(mic, 1, "mic1"))
+        root1 = tile([P, PACK, M], F32, "root1")
+        nc.sync.dma_start(out=pair_of(root1, 1), in_=pair_of(group_rows(power, 1), 1))
         for g in range(2):
-            for b in range(2):
-                cor_raw[b, g] = load_rows(cor[:, 512 * g : 512 * (g + 1)], b, f"cor{b}{g}")
-        gain_sb = tile([P, 2, 4], F32, "gain_sb")
-        nc.sync.dma_start(out=gain_sb[:], in_=gain.rearrange("(g p t) -> p g t", g=2, t=4))
-        prev_sb = [load_rows(prev, g, f"prev{g}") for g in range(2)]
+            cor_raw[1, g] = load_group(cor[:, PASS * g : PASS * (g + 1)], 1, f"cor1{g}")
+        gain_sb = tile([P, 2, PACK], F32, "gain_sb")
+        nc.sync.dma_start(out=gain_sb[:], in_=gain.rearrange("(g p t) -> p g t", g=2, t=PACK))
+        prev_sb = [load_group(prev, g, f"prev{g}") for g in range(2)]
 
         nc.vector.tensor_copy(v_sc[0][:], tab_sc[:].indirect(idx[:]))
         nc.scalar.dma_start(out=v_sc[1][0:112, :].bitcast(I32), in_=v_sc[0][4:116, :].bitcast(I32))
 
-        w4_dealt, w4_sc_dealt = [], []
-
-        def deal_w4(b, words_after=None, scales_after=None):
-            words = tile([P, 2, 4, 2 * P], U8, f"w4_dealt{b}", words_after)
+        def deal_w4(b, words_on=None, scales_on=None):
+            cols = slice(PASS * b, PASS * (b + 1))
+            words = tile([P, 2, PACK, 2 * P], U8, f"w4_dealt{b}", words_on)
             nc.vector.tensor_copy(
                 out=words[:].bitcast(U16),
-                in_=w4_raw[:].bitcast(U16)[:, :, 512 * b : 512 * (b + 1)].rearrange("p a (c i) -> p a i c", i=4),
+                in_=w4_raw[:].bitcast(U16)[:, :, cols].rearrange("p a (c i) -> p a i c", i=PACK),
             )
-            scales = tile([P, 2, 4, P], U8, f"w4_sc_dealt{b}", scales_after)
-            nc.vector.tensor_copy(
-                out=scales[:], in_=w4_sc[:, :, 512 * b : 512 * (b + 1)].rearrange("p a (c i) -> p a i c", i=4)
-            )
-            w4_dealt.append(words)
-            w4_sc_dealt.append(scales)
+            scales = tile([P, 2, PACK, P], U8, f"w4_sc_dealt{b}", scales_on)
+            nc.vector.tensor_copy(out=scales[:], in_=w4_sc[:, :, cols].rearrange("p a (c i) -> p a i c", i=PACK))
+            return words, scales
 
-        deal_w4(0)
+        w4_dealt = [deal_w4(0)]
         v = [tile([P, S], U32, f"v{a}") for a in range(2)]
         nc.vector.tensor_copy(v[0][:], tab[0][:].bitcast(U32).indirect(idx[:]))
         for half in range(2):
             nc.vector.tensor_copy(
                 v[1][:, BANK * half : BANK * (half + 1)],
-                tab[1][:].bitcast(U32).indirect(idx[:, 32 * half : 32 * (half + 1)]),
+                tab[1][:].bitcast(U32).indirect(idx[:, BANK // 16 * half : BANK // 16 * (half + 1)]),
             )
-        deal_w4(1, "tab1", "w4_raw")
+        w4_dealt.append(deal_w4(1, "tab1", "w4_raw"))
 
-        def on_power(func, b, pair):
-            part = power_sb[b][:, 2 * pair : 2 * pair + 2, :]
-            nc.scalar.activation(out=part, in_=part, func=func)
+        def inverse_root(out, in_):
+            nc.scalar.activation(out=out, in_=in_, func=ACT.Abs_reciprocal_sqrt)
+
+        def square(out, in_):
+            nc.scalar.activation(out=out, in_=in_, func=ACT.Square)
 
         h = {}
 
         def filter_rows(b, i):
-            rows = tile([P, S], F32, f"h{b}{i}")
+            words, scales = w4_dealt[b]
+            h[b, i] = tile([P, S], F32, f"h{b}{i}")
             for half in range(2):
                 cols = slice(BANK * half, BANK * (half + 1))
-                acc = psum.tile([P, BANK], F32, name="acc", tag=f"bank{2 * i + half}")
+                acc = psum.tile([P, BANK], F32, name="acc", tag=f"bank{(2 * (PACK * b + i) + half) % H_BANKS}")
                 for a in range(2):
                     nc.tensor.matmul_mx(
                         out=acc[:],
-                        lhsT=w4_dealt[b][:, a, i, :].bitcast(FP4X4),
-                        lhsT_scale=w4_sc_dealt[b][:, a, i, :],
+                        lhsT=words[:, a, i, :].bitcast(FP4X4),
+                        lhsT_scale=scales[:, a, i, :],
                         rhs=v[a][:, cols].bitcast(FP8X4),
                         rhs_scale=v_sc[a][:, cols],
                         start=(a == 0),
                         stop=(a == 1),
                     )
-                nc.scalar.copy(out=rows[:, cols], in_=acc[:])
-            h[b, i] = rows
+                nc.scalar.copy(out=h[b, i][:, cols], in_=acc[:])
 
-        x = {}
+        x = [tile([P, PACK, M], F32, f"x{b}") for b in range(2)]
 
         def pick(b, i):
-            if i == 0:
-                x[b] = tile([P, 4, M], F32, f"x{b}")
             nc.vector.tensor_tensor(x[b][:, i, :], h[b, i][:].indirect(idx2[:]), wgt_sb[:], ALU.mult)
 
-        z, z_codes, z_sc = {}, {}, {}
+        def subtract(b, on):
+            res = tile([P, PACK, M], F32, f"res{b}", on)
+            nc.vector.tensor_tensor(res[:], mic_sb[b][:], x[b][:], ALU.subtract)
+            return res
 
-        def residual(b):
-            nc.vector.tensor_tensor(x[b][:], mic_sb[b][:], x[b][:], ALU.subtract)
-            z[b] = tile([P, M, 4], BF16, f"z{b}")
-            nc.vector.tensor_tensor(
-                z[b][:].rearrange("p (c e) i -> p c i e", e=2),
-                x[b][:].rearrange("p i (c e) -> p c i e", e=2),
-                power_sb[b][:].rearrange("p i (c e) -> p c i e", e=2),
-                ALU.mult,
-            )
+        def by_pairs(rows):
+            return rows.rearrange("p i (c e) -> p c i e", e=2)
 
-        def quantize_z(b, after=None):
-            z_codes[b] = tile([P, M], U32, f"z_codes{b}", after)
-            z_sc[b] = tile([P, M], U8, f"z_sc{b}")
-            nc.vector.quantize_mx(
-                out=z_codes[b][:].bitcast(FP8X4), scales=z_sc[b][:], in_=z[b][:].rearrange("p m i -> p (m i)")
-            )
+        def words_by_pairs(words):
+            return words.rearrange("p (c e) i -> p c i e", e=2)
 
-        cor_codes, cor_sc = {}, {}
+        def normalize(b, res, inverse, on):
+            z = tile([P, M, PACK], BF16, f"z{b}", on)
+            nc.vector.tensor_tensor(words_by_pairs(z[:]), by_pairs(res[:]), by_pairs(inverse[:]), ALU.mult)
+            return z
 
-        def quantize_cor(b, g):
-            dealt = tile([P, 4, P, 4], BF16, f"cor_bf{b}{g}")
+        def quantize(values, name, on=None):
+            codes = tile([P, BANK], U32, f"{name}_codes", on)
+            scales = tile([P, BANK], U8, f"{name}_sc")
+            nc.vector.quantize_mx(out=codes[:].bitcast(FP8X4), scales=scales[:], in_=values)
+            return codes, scales
+
+        def quantize_z(b, z, on):
+            return quantize(z[:].rearrange("p m i -> p (m i)"), f"z{b}", on)
+
+        cor_mx = {}
+
+        def quantize_cor(b, g, dealt_on=None, codes_on=None):
+            dealt = tile([P, PACK, P, PACK], BF16, f"cor_bf{b}{g}", dealt_on)
             nc.scalar.copy(
-                out=dealt[:].rearrange("p t c j -> p c j t"),
-                in_=cor_raw[b, g][:].rearrange("p j (c t) -> p c j t", t=4),
+                out=dealt[:].rearrange("p (u e) c j -> p u c j e", e=2),
+                in_=cor_raw[b, g][:].rearrange("p j (c u e) -> p u c j e", u=2, e=2),
             )
-            codes = tile([P, BANK], U32, f"cor_codes{b}{g}")
-            scales = tile([P, BANK], U8, f"cor_sc{b}{g}")
-            nc.vector.quantize_mx(
-                out=codes[:].bitcast(FP8X4), scales=scales[:], in_=dealt[:].rearrange("p t c j -> p (t c j)")
-            )
-            cor_codes[b, g], cor_sc[b, g] = codes, scales
+            cor_mx[b, g] = quantize(dealt[:].rearrange("p t c j -> p (t c j)"), f"cor{b}{g}", codes_on)
 
-        on_power(ACT.Abs_reciprocal_sqrt, 0, 0)
-        on_power(ACT.Square, 0, 0)
-        on_power(ACT.Abs_reciprocal_sqrt, 0, 1)
-        for i in range(4):
+        inverse_root(pair_of(power0, 0), pair_of(power0, 0))
+        square(pair_of(power0, 0), pair_of(power0, 0))
+        for i in range(2):
+            inverse_root(root1[:, i, :], power1_early[i][:])
+        for i in range(PACK):
             filter_rows(0, i)
-        on_power(ACT.Square, 0, 1)
-        for i in range(4):
-            filter_rows(1, i)
-        for pair in range(2):
-            on_power(ACT.Abs_reciprocal_sqrt, 1, pair)
-            on_power(ACT.Square, 1, pair)
-        for i in range(4):
+        for i in range(PACK):
             pick(0, i)
-        residual(0)
-        for i in range(4):
-            pick(1, i)
-        quantize_z(0)
-        residual(1)
-        quantize_cor(0, 0)
+        filter_rows(1, 0)
+        filter_rows(1, 1)
+        root0 = tile([P, 2, M], F32, "root0", "h03")
+        inverse_root(root0[:], pair_of(power0, 1))
+        square(pair_of(power0, 1), root0[:])
+        filter_rows(1, 2)
+        filter_rows(1, 3)
+        pick(1, 0)
+        res0 = subtract(0, "h10")
+        pick(1, 1)
+        z0 = normalize(0, res0, power0, "h11")
+        pick(1, 2)
+        z_mx = [quantize_z(0, z0, "h12")]
+        pick(1, 3)
+        quantize_cor(0, 0, dealt_on="v0")
+        res1 = subtract(1, "v0")
+        quantize_cor(0, 1, dealt_on="v1")
+        inverse_root(pair_of(root1, 1), pair_of(root1, 1))
+        inverse1 = tile([P, PACK, M], F32, "inverse1", "mic0")
+        square(inverse1[:], root1[:])
+        z1 = normalize(1, res1, inverse1, "v1")
         quantize_cor(1, 0)
-        quantize_z(1, "cor_bf10")
-        quantize_cor(0, 1)
-        quantize_cor(1, 1)
+        z_mx.append(quantize_z(1, z1, "cor_bf10"))
+        quantize_cor(1, 1, codes_on="v1")
 
-        def step(g, t):
-            acc = psum.tile([P, BANK], F32, name="acc", tag=f"bank{4 * g + t}")
-            cols = slice(P * t, P * (t + 1))
-            for b in range(2):
-                nc.tensor.matmul_mx(
-                    out=acc[:],
-                    lhsT=cor_codes[b, g][:, cols].bitcast(FP8X4),
-                    lhsT_scale=cor_sc[b, g][:, cols],
-                    rhs=z_codes[b][:].bitcast(FP8X4),
-                    rhs_scale=z_sc[b][:],
-                    start=(b == 0),
-                    stop=(b == 1),
+        y = [prev_sb[0], tile([P, PACK, M], F32, "y1", "cor_bf11")]
+        for t in range(PACK):
+            nc.scalar.activation(
+                out=y[0][:, t, :], in_=prev_sb[0][:, t, :], func=ACT.Copy, scale=gain_sb[:, 0, t : t + 1]
+            )
+        for t in range(PACK):
+            nc.gpsimd.tensor_scalar(y[1][:, t, :], prev_sb[1][:, t, :], gain_sb[:, 1, t : t + 1], 0.0, ALU.mult, ALU.add)
+
+        for g in range(2):
+            for t in range(PACK):
+                acc = psum.tile([P, BANK], F32, name="acc", tag=f"bank{PACK * g + t}")
+                cols = slice(P * t, P * (t + 1))
+                for b in range(2):
+                    nc.tensor.matmul_mx(
+                        out=acc[:],
+                        lhsT=cor_mx[b, g][0][:, cols].bitcast(FP8X4),
+                        lhsT_scale=cor_mx[b, g][1][:, cols],
+                        rhs=z_mx[b][0][:].bitcast(FP8X4),
+                        rhs_scale=z_mx[b][1][:],
+                        start=(b == 0),
+                        stop=(b == 1),
+                    )
+                nc.vector.scalar_tensor_tensor(
+                    y[g][:, t, :], acc[:], gain_sb[:, g, t : t + 1], y[g][:, t, :], ALU.mult, ALU.add
                 )
-            return acc
+                if t % 2:
+                    nc.sync.dma_start(out=pair_of(group_rows(out_0, g), t // 2), in_=pair_of(y[g], t // 2))
 
-        def store_y(g, y, t0, t1):
-            rows = out_0[512 * g : 512 * (g + 1), :].rearrange("(p t) m -> p t m", t=4)
-            nc.sync.dma_start(out=rows[:, t0:t1, :], in_=y[:, t0:t1, :])
+        y_bf = [tile([P, M, PACK], BF16, f"y_bf{g}") for g in range(2)]
 
-        y0 = prev_sb[0]
-        for t in range(4):
-            acc = step(0, t)
-            nc.vector.tensor_tensor(y0[:, t, :], acc[:], y0[:, t, :], ALU.add)
-            nc.scalar.activation(out=y0[:, t, :], in_=y0[:, t, :], func=ACT.Copy, scale=gain_sb[:, 0, t : t + 1])
-            if t % 2:
-                store_y(0, y0, t - 1, t + 1)
-        y1 = tile([P, 4, M], F32, "y1", "cor_bf11")
-        for t in range(4):
-            nc.gpsimd.tensor_scalar(y1[:, t, :], prev_sb[1][:, t, :], gain_sb[:, 1, t : t + 1], 0.0, ALU.mult, ALU.add)
-        for t in range(4):
-            acc = step(1, t)
-            nc.vector.scalar_tensor_tensor(y1[:, t, :], acc[:], gain_sb[:, 1, t : t + 1], y1[:, t, :], ALU.mult, ALU.add)
-            if t % 2:
-                store_y(1, y1, t - 1, t + 1)
+        def round_y(copy, g, cols):
+            copy(out=words_by_pairs(y_bf[g][:, cols, :]), in_=by_pairs(y[g][:, :, cols]))
 
+        round_y(nc.scalar.copy, 0, slice(0, M))
+        round_y(nc.scalar.copy, 1, slice(0, SCALAR_COLS))
+        round_y(nc.vector.tensor_copy, 1, slice(SCALAR_COLS, M))
         y_sc = tile([P, 2, M], U8, "y_sc")
-        y_bf = [tile([P, M, 4], BF16, f"y_bf{g}") for g in range(2)]
-        nc.scalar.copy(
-            out=y_bf[0][:].rearrange("p (c e) t -> p c t e", e=2), in_=y0[:].rearrange("p t (c e) -> p c t e", e=2)
-        )
-        nc.vector.tensor_copy(
-            out=y_bf[1][:].rearrange("p (c e) t -> p c t e", e=2), in_=y1[:].rearrange("p t (c e) -> p c t e", e=2)
-        )
         for g in range(2):
             codes = tile([P, M], I32, f"y_codes{g}")
             nc.vector.quantize_mx(

@@ -184,10 +184,16 @@ def tile_list_subband_echo_update_kernel(
 
         def quantize_cor(b, g, dealt_on=None, codes_on=None):
             dealt = tile([P, PACK, P, PACK], BF16, f"cor_bf{b}{g}", dealt_on)
-            nc.scalar.copy(
-                out=dealt[:].rearrange("p (u e) c j -> p u c j e", e=2),
-                in_=cor_raw[b, g][:].rearrange("p j (c u e) -> p u c j e", u=2, e=2),
-            )
+            if (b, g) == (0, 0):
+                nc.vector.tensor_copy(
+                    out=dealt[:].rearrange("p (u e) c j -> p u c j e", e=2),
+                    in_=cor_raw[b, g][:].rearrange("p j (c u e) -> p u c j e", u=2, e=2),
+                )
+            else:
+                nc.scalar.copy(
+                    out=dealt[:].rearrange("p t c j -> p c j t"),
+                    in_=cor_raw[b, g][:].rearrange("p j (c t) -> p c j t", t=PACK),
+                )
             cor_mx[b, g] = quantize(dealt[:].rearrange("p t c j -> p (t c j)"), f"cor{b}{g}", codes_on)
 
         inverse_root(pair_of(power0, 0), pair_of(power0, 0))

@@ -1,6 +1,7 @@
 from contextlib import ExitStack
 
 import concourse.mybir as mybir
+from concourse.masks import make_identity
 
 K, T, S, M, H, N = 1024, 2048, 1024, 512, 1024, 1024
 FLOPS = 2 * K * H * S + 2 * H * N * M
@@ -20,8 +21,11 @@ P = 128
 PACK = 4
 PASS = P * PACK
 BANK = 512
-H_BANKS = 3
+BANKS = 8
+BLOCKS = M // P
+EARLY_ROWS = 2
 SCALAR_COLS = 192
+RUN = 4
 
 
 def tile_list_subband_echo_update_kernel(
@@ -35,6 +39,9 @@ def tile_list_subband_echo_update_kernel(
 
         def tile(shape, dtype, name, on=None):
             return sbuf.tile(shape, dtype, name=name, tag=on or name, align_bytes=64)
+
+        def bank(number):
+            return psum.tile([P, BANK], F32, name="acc", tag=f"bank{number % BANKS}")
 
         def group_rows(src, b):
             return src[PASS * b : PASS * (b + 1), :].rearrange("(p i) m -> p i m", i=PACK)
@@ -58,11 +65,19 @@ def tile_list_subband_echo_update_kernel(
         warm = tile([P, 1], F32, "warm")
         nc.scalar.activation(out=warm[:], in_=one[:], func=ACT.Abs_reciprocal_sqrt)
 
-        w4_raw = tile([P, 2, H // 2], I32, "w4_raw")
-        nc.sync.dma_start(out=w4_raw[:], in_=w4_words.bitcast(I32).rearrange("a p c -> p a c"))
-        for q in range(4):
+        ident = tile([P, P], F32, "ident")
+        make_identity(nc, ident[:])
+
+        def load_w4(b):
+            words = tile([P, 2, PASS // 2], I32, f"w4_raw{b}")
+            cols = slice(PASS // 2 * b, PASS // 2 * (b + 1))
+            nc.sync.dma_start(out=words[:], in_=w4_words.bitcast(I32)[:, :, cols].rearrange("a p c -> p a c"))
+            return words
+
+        w4_raw = [load_w4(0)]
+        for r in range(4):
             nc.sync.dma_start(
-                out=tab_sc[32 * q : 32 * q + 8, :].bitcast(I32), in_=tab_scales[:, 4 * q : 4 * q + 4, :].bitcast(I32)
+                out=tab_sc[r:P:16, :].bitcast(I32), in_=tab_scales[:, r:16:4, :].bitcast(I32).rearrange("a q c -> q a c")
             )
         idx = lists.tile([P, S // 16], U16, name="idx")
         nc.sync.dma_start(idx[:], offs)
@@ -73,42 +88,40 @@ def tile_list_subband_echo_update_kernel(
             return words
 
         tab = [load_table(0)]
-        power0 = tile([P, PACK, M], F32, "power0")
-        nc.sync.dma_start(out=pair_of(power0, 0), in_=pair_of(group_rows(power, 0), 0))
+        power_sb = [tile([P, PACK, M], F32, "power0")]
+        nc.sync.dma_start(out=power_sb[0][:, 0, :], in_=group_rows(power, 0)[:, 0, :])
         for q in range(4):
             nc.sync.dma_start(
                 out=w4_sc[32 * q : 32 * q + 4, :, :].bitcast(I32),
                 in_=w4_scales[:, 4 * q : 4 * q + 4, :].bitcast(I32).rearrange("a r c -> r a c"),
             )
         tab.append(load_table(1))
-        power1_early = [tile([P, M], F32, f"power1_early{i}", f"h0{i}") for i in range(2)]
-        for i in range(2):
-            nc.sync.dma_start(out=power1_early[i][:], in_=group_rows(power, 1)[:, i, :])
+        nc.sync.dma_start(out=power_sb[0][:, 1, :], in_=group_rows(power, 0)[:, 1, :])
+        w4_raw.append(load_w4(1))
         idx2 = lists.tile([P, M // 16], U16, name="idx2")
         nc.sync.dma_start(idx2[:], offs2)
         wgt_sb = tile([P, M], F32, "wgt_sb")
         nc.sync.dma_start(out=wgt_sb[:], in_=wgt)
-        nc.sync.dma_start(out=pair_of(power0, 1), in_=pair_of(group_rows(power, 0), 1))
-        mic_sb = [load_group(mic, 0, "mic0")]
-        cor_raw = {(0, g): load_group(cor[:, PASS * g : PASS * (g + 1)], 0, f"cor0{g}") for g in range(2)}
-        mic_sb.append(load_group(mic, 1, "mic1"))
-        root1 = tile([P, PACK, M], F32, "root1")
-        nc.sync.dma_start(out=pair_of(root1, 1), in_=pair_of(group_rows(power, 1), 1))
-        for g in range(2):
-            cor_raw[1, g] = load_group(cor[:, PASS * g : PASS * (g + 1)], 1, f"cor1{g}")
+
+        def load_cor(b, g):
+            return load_group(cor[:, PASS * g : PASS * (g + 1)], b, f"cor{b}{g}")
+
+        nc.sync.dma_start(out=pair_of(power_sb[0], 1), in_=pair_of(group_rows(power, 0), 1))
+        mic_sb = [load_group(mic, b, f"mic{b}") for b in range(2)]
+        power_sb.append(load_group(power, 1, "power1"))
+        cor_raw = {(b, g): load_cor(b, g) for b in range(2) for g in range(2)}
         gain_sb = tile([P, 2, PACK], F32, "gain_sb")
         nc.sync.dma_start(out=gain_sb[:], in_=gain.rearrange("(g p t) -> p g t", g=2, t=PACK))
         prev_sb = [load_group(prev, g, f"prev{g}") for g in range(2)]
 
         nc.vector.tensor_copy(v_sc[0][:], tab_sc[:].indirect(idx[:]))
-        nc.scalar.dma_start(out=v_sc[1][0:112, :].bitcast(I32), in_=v_sc[0][4:116, :].bitcast(I32))
+        nc.scalar.dma_start(out=v_sc[1][0:112, :].bitcast(I32), in_=v_sc[0][16:128, :].bitcast(I32))
 
         def deal_w4(b, words_on=None, scales_on=None):
             cols = slice(PASS * b, PASS * (b + 1))
             words = tile([P, 2, PACK, 2 * P], U8, f"w4_dealt{b}", words_on)
             nc.vector.tensor_copy(
-                out=words[:].bitcast(U16),
-                in_=w4_raw[:].bitcast(U16)[:, :, cols].rearrange("p a (c i) -> p a i c", i=PACK),
+                out=words[:].bitcast(U16), in_=w4_raw[b][:].bitcast(U16).rearrange("p a (c i) -> p a i c", i=PACK)
             )
             scales = tile([P, 2, PACK, P], U8, f"w4_sc_dealt{b}", scales_on)
             nc.vector.tensor_copy(out=scales[:], in_=w4_sc[:, :, cols].rearrange("p a (c i) -> p a i c", i=PACK))
@@ -122,7 +135,7 @@ def tile_list_subband_echo_update_kernel(
                 v[1][:, BANK * half : BANK * (half + 1)],
                 tab[1][:].bitcast(U32).indirect(idx[:, BANK // 16 * half : BANK // 16 * (half + 1)]),
             )
-        w4_dealt.append(deal_w4(1, "tab1", "w4_raw"))
+        w4_dealt.append(deal_w4(1, "tab1", "w4_raw1"))
 
         def inverse_root(out, in_):
             nc.scalar.activation(out=out, in_=in_, func=ACT.Abs_reciprocal_sqrt)
@@ -137,7 +150,7 @@ def tile_list_subband_echo_update_kernel(
             h[b, i] = tile([P, S], F32, f"h{b}{i}")
             for half in range(2):
                 cols = slice(BANK * half, BANK * (half + 1))
-                acc = psum.tile([P, BANK], F32, name="acc", tag=f"bank{(2 * (PACK * b + i) + half) % H_BANKS}")
+                acc = bank(EARLY_ROWS + 2 * (PACK * b + i) + half)
                 for a in range(2):
                     nc.tensor.matmul_mx(
                         out=acc[:],
@@ -148,9 +161,9 @@ def tile_list_subband_echo_update_kernel(
                         start=(a == 0),
                         stop=(a == 1),
                     )
-                nc.scalar.copy(out=h[b, i][:, cols], in_=acc[:])
+                nc.scalar.activation(out=h[b, i][:, cols], in_=acc[:], func=ACT.Copy, scale=(-1.0, 1.0)[b])
 
-        x = [tile([P, PACK, M], F32, f"x{b}") for b in range(2)]
+        x = [tile([P, PACK, M], F32, "x0", "tab0"), tile([P, PACK, M], F32, "x1")]
 
         def pick(b, i):
             nc.vector.tensor_tensor(x[b][:, i, :], h[b, i][:].indirect(idx2[:]), wgt_sb[:], ALU.mult)
@@ -161,10 +174,10 @@ def tile_list_subband_echo_update_kernel(
             return res
 
         def by_pairs(rows):
-            return rows.rearrange("p i (c e) -> p c i e", e=2)
+            return rows.rearrange("p i (c e) -> p c i e", e=RUN)
 
         def words_by_pairs(words):
-            return words.rearrange("p (c e) i -> p c i e", e=2)
+            return words.rearrange("p (c e) i -> p c i e", e=RUN)
 
         def normalize(b, res, inverse, on):
             z = tile([P, M, PACK], BF16, f"z{b}", on)
@@ -180,54 +193,122 @@ def tile_list_subband_echo_update_kernel(
         def quantize_z(b, z, on):
             return quantize(z[:].rearrange("p m i -> p (m i)"), f"z{b}", on)
 
+        cor_bf = {}
         cor_mx = {}
 
-        def quantize_cor(b, g, dealt_on=None, codes_on=None):
-            dealt = tile([P, PACK, P, PACK], BF16, f"cor_bf{b}{g}", dealt_on)
-            if (b, g) == (0, 0):
+        def round_cor(b, g, engine, on=None):
+            dealt = tile([P, PACK, P, PACK], BF16, f"cor_bf{b}{g}", on)
+            cor_bf[b, g] = dealt
+            raw = cor_raw[b, g][:].rearrange("p j (c t) -> p j c t", t=PACK)
+            if engine == "vector":
                 nc.vector.tensor_copy(
                     out=dealt[:].rearrange("p (u e) c j -> p u c j e", e=2),
-                    in_=cor_raw[b, g][:].rearrange("p j (c u e) -> p u c j e", u=2, e=2),
+                    in_=raw.rearrange("p j c (u e) -> p u c j e", e=2),
                 )
+            elif engine == "scalar":
+                nc.scalar.copy(out=dealt[:].rearrange("p t c j -> p c j t"), in_=raw.rearrange("p j c t -> p c j t"))
             else:
-                nc.scalar.copy(
-                    out=dealt[:].rearrange("p t c j -> p c j t"),
-                    in_=cor_raw[b, g][:].rearrange("p j (c t) -> p c j t", t=PACK),
+                nc.gpsimd.tensor_scalar(
+                    dealt[:].rearrange("p t c j -> p c t j"),
+                    raw.rearrange("p j c t -> p c t j"),
+                    1.0,
+                    0.0,
+                    ALU.mult,
+                    ALU.add,
                 )
-            cor_mx[b, g] = quantize(dealt[:].rearrange("p t c j -> p (t c j)"), f"cor{b}{g}", codes_on)
 
-        inverse_root(pair_of(power0, 0), pair_of(power0, 0))
-        square(pair_of(power0, 0), pair_of(power0, 0))
-        for i in range(2):
-            inverse_root(root1[:, i, :], power1_early[i][:])
-        for i in range(PACK):
-            filter_rows(0, i)
-        for i in range(PACK):
-            pick(0, i)
-        filter_rows(1, 0)
-        filter_rows(1, 1)
-        root0 = tile([P, 2, M], F32, "root0", "h03")
-        inverse_root(root0[:], pair_of(power0, 1))
-        square(pair_of(power0, 1), root0[:])
-        filter_rows(1, 2)
-        filter_rows(1, 3)
-        pick(1, 0)
-        res0 = subtract(0, "h10")
-        pick(1, 1)
-        z0 = normalize(0, res0, power0, "h11")
-        pick(1, 2)
-        z_mx = [quantize_z(0, z0, "h12")]
-        pick(1, 3)
-        quantize_cor(0, 0, dealt_on="v0")
-        res1 = subtract(1, "v0")
-        quantize_cor(0, 1, dealt_on="v1")
-        inverse_root(pair_of(root1, 1), pair_of(root1, 1))
-        inverse1 = tile([P, PACK, M], F32, "inverse1", "mic0")
-        square(inverse1[:], root1[:])
-        z1 = normalize(1, res1, inverse1, "v1")
-        quantize_cor(1, 0)
-        z_mx.append(quantize_z(1, z1, "cor_bf10"))
-        quantize_cor(1, 1, codes_on="v1")
+        def quantize_cor(b, g, on=None):
+            cor_mx[b, g] = quantize(cor_bf[b, g][:].rearrange("p t c j -> p (t c j)"), f"cor{b}{g}", on)
+
+        def turned_cols(i):
+            place = 2 * (i % 2) + i // 2
+            return slice(P * place, P * (place + 1))
+
+        def block(rows, i, blk):
+            return rows[:, i, P * blk : P * (blk + 1)]
+
+        inverse0 = tile([P, BLOCKS, BANK], F32, "inverse0")
+
+        roots = {}
+
+        def turned_root(i):
+            acc = bank(i)
+            for blk in range(BLOCKS):
+                nc.tensor.transpose(acc[:, P * blk : P * (blk + 1)], block(power_sb[0], i, blk), ident[:])
+            roots[i] = tile([P, BANK], F32, f"root0{i}")
+            inverse_root(roots[i][:], acc[:])
+
+        def square_turned(i):
+            square(inverse0[:, :, turned_cols(i)], roots[i][:].rearrange("p (k c) -> p k c", k=BLOCKS))
+
+        z_turned = {}
+
+        def normalize_turned(blk):
+            acc = bank(BLOCKS + blk)
+            for n, rows in enumerate((mic_sb[0], x[0])):
+                for i in range(PACK):
+                    nc.tensor.matmul(
+                        acc[:, turned_cols(i)],
+                        block(rows, i, blk),
+                        ident[:],
+                        start=(n == 0 and i == 0),
+                        stop=(n == 1 and i == PACK - 1),
+                        is_transpose=True,
+                    )
+            z_turned[blk] = tile([P, BANK], BF16, f"z_turned{blk}")
+            nc.vector.tensor_tensor(
+                z_turned[blk][:].rearrange("p (c d e) -> p c e d", d=2, e=2),
+                acc[:].rearrange("p (e c d) -> p c e d", e=2, d=2),
+                inverse0[:, blk, :].rearrange("p (e c d) -> p c e d", e=2, d=2),
+                ALU.mult,
+            )
+
+        z0 = tile([P, M, PACK], BF16, "z0", "v0")
+
+        def turn_back(half):
+            acc = bank(half)
+            for j in range(2):
+                words = z_turned[2 * half + j][:].bitcast(F32)
+                for u in range(2):
+                    at = 2 * P * u + P * j
+                    nc.tensor.transpose(acc[:, at : at + P], words[:, P * u : P * (u + 1)], ident[:])
+            nc.scalar.copy(
+                out=z0[:, 2 * P * half : 2 * P * (half + 1), :].bitcast(F32).rearrange("p (c d) u -> p c u d", d=2),
+                in_=acc[:].rearrange("p (u c d) -> p c u d", u=2, d=2),
+            )
+
+        turned_root(0)
+        square_turned(0)
+        turned_root(1)
+        for b in range(2):
+            for i in range(PACK):
+                filter_rows(b, i)
+                pick(b, i)
+        for i in range(EARLY_ROWS, PACK):
+            turned_root(i)
+        for i in range(1, PACK):
+            square_turned(i)
+        root1 = [tile([P, 2, M], F32, f"root1{pair}", f"root0{2 + pair}") for pair in range(2)]
+        for pair in range(2):
+            inverse_root(root1[pair][:], pair_of(power_sb[1], pair))
+        for pair in range(2):
+            square(pair_of(power_sb[1], pair), root1[pair][:])
+        res1 = subtract(1, "tab1")
+        round_cor(0, 0, "gpsimd", "x1")
+        for blk in range(BLOCKS):
+            normalize_turned(blk)
+        turn_back(0)
+        turn_back(1)
+        round_cor(0, 1, "scalar", "root03")
+        round_cor(1, 1, "scalar")
+        quantize_cor(0, 0, "inverse0")
+        z1 = normalize(1, res1, power_sb[1], "x1")
+        z_mx = [quantize_z(0, z0, "tab1")]
+        round_cor(1, 0, "vector", "v0")
+        quantize_cor(0, 1, "cor10")
+        z_mx.append(quantize_z(1, z1, "root03"))
+        quantize_cor(1, 0, "x1")
+        quantize_cor(1, 1, "v0")
 
         y = [prev_sb[0], tile([P, PACK, M], F32, "y1", "cor_bf11")]
         for t in range(PACK):
@@ -237,27 +318,37 @@ def tile_list_subband_echo_update_kernel(
         for t in range(PACK):
             nc.gpsimd.tensor_scalar(y[1][:, t, :], prev_sb[1][:, t, :], gain_sb[:, 1, t : t + 1], 0.0, ALU.mult, ALU.add)
 
+        def product(acc, b, g, t):
+            cols = slice(P * t, P * (t + 1))
+            nc.tensor.matmul_mx(
+                out=acc[:],
+                lhsT=cor_mx[b, g][0][:, cols].bitcast(FP8X4),
+                lhsT_scale=cor_mx[b, g][1][:, cols],
+                rhs=z_mx[b][0][:].bitcast(FP8X4),
+                rhs_scale=z_mx[b][1][:],
+                start=(b == 0),
+                stop=(b == 1),
+            )
+
+        accs = {}
+
+        def first_pass(g):
+            for t in range(PACK):
+                accs[g, t] = bank(2 + PACK * g + t)
+                product(accs[g, t], 0, g, t)
+
+        first_pass(0)
+        first_pass(1)
         for g in range(2):
             for t in range(PACK):
-                acc = psum.tile([P, BANK], F32, name="acc", tag=f"bank{PACK * g + t}")
-                cols = slice(P * t, P * (t + 1))
-                for b in range(2):
-                    nc.tensor.matmul_mx(
-                        out=acc[:],
-                        lhsT=cor_mx[b, g][0][:, cols].bitcast(FP8X4),
-                        lhsT_scale=cor_mx[b, g][1][:, cols],
-                        rhs=z_mx[b][0][:].bitcast(FP8X4),
-                        rhs_scale=z_mx[b][1][:],
-                        start=(b == 0),
-                        stop=(b == 1),
-                    )
+                product(accs[g, t], 1, g, t)
                 nc.vector.scalar_tensor_tensor(
-                    y[g][:, t, :], acc[:], gain_sb[:, g, t : t + 1], y[g][:, t, :], ALU.mult, ALU.add
+                    y[g][:, t, :], accs[g, t][:], gain_sb[:, g, t : t + 1], y[g][:, t, :], ALU.mult, ALU.add
                 )
                 if t % 2:
                     nc.sync.dma_start(out=pair_of(group_rows(out_0, g), t // 2), in_=pair_of(y[g], t // 2))
 
-        y_bf = [tile([P, M, PACK], BF16, f"y_bf{g}") for g in range(2)]
+        y_bf = [tile([P, M, PACK], BF16, f"y_bf{g}", f"h0{g}") for g in range(2)]
 
         def round_y(copy, g, cols):
             copy(out=words_by_pairs(y_bf[g][:, cols, :]), in_=by_pairs(y[g][:, :, cols]))

@@ -24,7 +24,7 @@ BANK = 512
 BANKS = 8
 BLOCKS = M // P
 EARLY_ROWS = 2
-SCALAR_COLS = 192
+SCALAR_COLS = 256
 RUN = 4
 
 
@@ -135,7 +135,7 @@ def tile_list_subband_echo_update_kernel(
                 v[1][:, BANK * half : BANK * (half + 1)],
                 tab[1][:].bitcast(U32).indirect(idx[:, BANK // 16 * half : BANK // 16 * (half + 1)]),
             )
-        w4_dealt.append(deal_w4(1, "tab1", "w4_raw1"))
+        w4_dealt.append(deal_w4(1, None, "tab1"))
 
         def inverse_root(out, in_):
             nc.scalar.activation(out=out, in_=in_, func=ACT.Abs_reciprocal_sqrt)
@@ -170,7 +170,8 @@ def tile_list_subband_echo_update_kernel(
 
         def subtract(b, on):
             res = tile([P, PACK, M], F32, f"res{b}", on)
-            nc.vector.tensor_tensor(res[:], mic_sb[b][:], x[b][:], ALU.subtract)
+            for pair in range(2):
+                nc.vector.tensor_tensor(pair_of(res, pair), pair_of(mic_sb[b], pair), pair_of(x[b], pair), ALU.subtract)
             return res
 
         def by_pairs(rows):
@@ -301,14 +302,14 @@ def tile_list_subband_echo_update_kernel(
         turn_back(1)
         round_cor(0, 1, "scalar", "root03")
         round_cor(1, 1, "scalar")
-        quantize_cor(0, 0, "inverse0")
-        z1 = normalize(1, res1, power_sb[1], "x1")
-        z_mx = [quantize_z(0, z0, "tab1")]
-        round_cor(1, 0, "vector", "v0")
-        quantize_cor(0, 1, "cor10")
-        z_mx.append(quantize_z(1, z1, "root03"))
-        quantize_cor(1, 0, "x1")
-        quantize_cor(1, 1, "v0")
+        quantize_cor(0, 0, "h02")
+        z1 = normalize(1, res1, power_sb[1], None)
+        z_mx = [quantize_z(0, z0, "h03")]
+        round_cor(1, 0, "vector", "v1")
+        quantize_cor(0, 1, "h10")
+        z_mx.append(quantize_z(1, z1, "h11"))
+        quantize_cor(1, 0, "h12")
+        quantize_cor(1, 1, "h13")
 
         y = [prev_sb[0], tile([P, PACK, M], F32, "y1", "cor_bf11")]
         for t in range(PACK):

@@ -23,7 +23,8 @@ PASS = P * PACK
 BANK = 512
 BANKS = 8
 BLOCKS = M // P
-EARLY_ROWS = 2
+EARLY_ROWS = 1
+AHEAD = 3
 SCALAR_COLS = 256
 RUN = 4
 
@@ -96,7 +97,6 @@ def tile_list_subband_echo_update_kernel(
                 in_=w4_scales[:, 4 * q : 4 * q + 4, :].bitcast(I32).rearrange("a r c -> r a c"),
             )
         tab.append(load_table(1))
-        nc.sync.dma_start(out=power_sb[0][:, 1, :], in_=group_rows(power, 0)[:, 1, :])
         w4_raw.append(load_w4(1))
         idx2 = lists.tile([P, M // 16], U16, name="idx2")
         nc.sync.dma_start(idx2[:], offs2)
@@ -106,7 +106,7 @@ def tile_list_subband_echo_update_kernel(
         def load_cor(b, g):
             return load_group(cor[:, PASS * g : PASS * (g + 1)], b, f"cor{b}{g}")
 
-        nc.sync.dma_start(out=pair_of(power_sb[0], 1), in_=pair_of(group_rows(power, 0), 1))
+        nc.sync.dma_start(out=power_sb[0][:, 1:PACK, :], in_=group_rows(power, 0)[:, 1:PACK, :])
         mic_sb = [load_group(mic, b, f"mic{b}") for b in range(2)]
         power_sb.append(load_group(power, 1, "power1"))
         cor_raw = {(b, g): load_cor(b, g) for b in range(2) for g in range(2)}
@@ -145,23 +145,38 @@ def tile_list_subband_echo_update_kernel(
 
         h = {}
 
-        def filter_rows(b, i):
+        h_acc = {}
+
+        def filter_pass(a, b, i, half):
             words, scales = w4_dealt[b]
-            h[b, i] = tile([P, S], F32, f"h{b}{i}")
+            cols = slice(BANK * half, BANK * (half + 1))
+            if a == 0:
+                h_acc[b, i, half] = bank(EARLY_ROWS + 2 * (PACK * b + i) + half)
+            nc.tensor.matmul_mx(
+                out=h_acc[b, i, half][:],
+                lhsT=words[:, a, i, :].bitcast(FP4X4),
+                lhsT_scale=scales[:, a, i, :],
+                rhs=v[a][:, cols].bitcast(FP8X4),
+                rhs_scale=v_sc[a][:, cols],
+                start=(a == 0),
+                stop=(a == 1),
+            )
+
+        def finish_half(b, i, half):
+            filter_pass(1, b, i, half)
+            if half == 0:
+                h[b, i] = tile([P, S], F32, f"h{b}{i}")
+            nc.scalar.activation(
+                out=h[b, i][:, BANK * half : BANK * (half + 1)],
+                in_=h_acc[b, i, half][:],
+                func=ACT.Copy,
+                scale=(-1.0, 1.0)[b],
+            )
+
+        def filter_rows(b, i):
             for half in range(2):
-                cols = slice(BANK * half, BANK * (half + 1))
-                acc = bank(EARLY_ROWS + 2 * (PACK * b + i) + half)
-                for a in range(2):
-                    nc.tensor.matmul_mx(
-                        out=acc[:],
-                        lhsT=words[:, a, i, :].bitcast(FP4X4),
-                        lhsT_scale=scales[:, a, i, :],
-                        rhs=v[a][:, cols].bitcast(FP8X4),
-                        rhs_scale=v_sc[a][:, cols],
-                        start=(a == 0),
-                        stop=(a == 1),
-                    )
-                nc.scalar.activation(out=h[b, i][:, cols], in_=acc[:], func=ACT.Copy, scale=(-1.0, 1.0)[b])
+                filter_pass(0, b, i, half)
+                finish_half(b, i, half)
 
         x = [tile([P, PACK, M], F32, "x0", "tab0"), tile([P, PACK, M], F32, "x1")]
 
@@ -280,10 +295,19 @@ def tile_list_subband_echo_update_kernel(
 
         turned_root(0)
         square_turned(0)
-        turned_root(1)
+        for i in range(AHEAD):
+            for half in range(2):
+                filter_pass(0, 0, i, half)
+        for half in range(2):
+            for i in range(2):
+                finish_half(0, i, half)
+        for i in range(2, AHEAD):
+            for half in range(2):
+                finish_half(0, i, half)
         for b in range(2):
             for i in range(PACK):
-                filter_rows(b, i)
+                if PACK * b + i >= AHEAD:
+                    filter_rows(b, i)
                 pick(b, i)
         for i in range(EARLY_ROWS, PACK):
             turned_root(i)
@@ -305,7 +329,7 @@ def tile_list_subband_echo_update_kernel(
         quantize_cor(0, 0, "h02")
         z1 = normalize(1, res1, power_sb[1], None)
         z_mx = [quantize_z(0, z0, "h03")]
-        round_cor(1, 0, "vector", "v1")
+        round_cor(1, 0, "vector", "tab1")
         quantize_cor(0, 1, "h10")
         z_mx.append(quantize_z(1, z1, "h11"))
         quantize_cor(1, 0, "h12")

@@ -25,6 +25,8 @@ BANKS = 8
 BLOCKS = M // P
 EARLY_ROWS = 1
 AHEAD = 3
+HALF = M // 2
+SCALAR_ROWS = 4
 SCALAR_COLS = 256
 RUN = 4
 
@@ -178,15 +180,25 @@ def tile_list_subband_echo_update_kernel(
                 filter_pass(0, b, i, half)
                 finish_half(b, i, half)
 
-        x = [tile([P, PACK, M], F32, "x0", "tab0"), tile([P, PACK, M], F32, "x1")]
+        x0 = tile([P, PACK, M], F32, "x0", "tab0")
+        x1 = [tile([P, PACK, HALF], F32, f"x1{half}") for half in range(2)]
+
+        def half_cols(half):
+            return slice(HALF * half, HALF * (half + 1))
 
         def pick(b, i):
-            nc.vector.tensor_tensor(x[b][:, i, :], h[b, i][:].indirect(idx2[:]), wgt_sb[:], ALU.mult)
+            if b == 0:
+                nc.vector.tensor_tensor(x0[:, i, :], h[b, i][:].indirect(idx2[:]), wgt_sb[:], ALU.mult)
+            else:
+                for half in range(2):
+                    entries = idx2[:, HALF // 16 * half : HALF // 16 * (half + 1)]
+                    nc.vector.tensor_tensor(
+                        x1[half][:, i, :], h[b, i][:].indirect(entries), wgt_sb[:, half_cols(half)], ALU.mult
+                    )
 
-        def subtract(b, on):
-            res = tile([P, PACK, M], F32, f"res{b}", on)
-            for pair in range(2):
-                nc.vector.tensor_tensor(pair_of(res, pair), pair_of(mic_sb[b], pair), pair_of(x[b], pair), ALU.subtract)
+        def subtract(engine, half, on):
+            res = tile([P, PACK, HALF], F32, f"res1{half}", on)
+            engine.tensor_tensor(res[:], mic_sb[1][:, :, half_cols(half)], x1[half][:], ALU.subtract)
             return res
 
         def by_pairs(rows):
@@ -195,10 +207,13 @@ def tile_list_subband_echo_update_kernel(
         def words_by_pairs(words):
             return words.rearrange("p (c e) i -> p c i e", e=RUN)
 
-        def normalize(b, res, inverse, on):
-            z = tile([P, M, PACK], BF16, f"z{b}", on)
-            nc.vector.tensor_tensor(words_by_pairs(z[:]), by_pairs(res[:]), by_pairs(inverse[:]), ALU.mult)
-            return z
+        z1 = tile([P, M, PACK], BF16, "z1")
+
+        def normalize(half, res):
+            cols = half_cols(half)
+            nc.vector.tensor_tensor(
+                words_by_pairs(z1[:, cols, :]), by_pairs(res[:]), by_pairs(power_sb[1][:, :, cols]), ALU.mult
+            )
 
         def quantize(values, name, on=None):
             codes = tile([P, BANK], U32, f"{name}_codes", on)
@@ -221,17 +236,8 @@ def tile_list_subband_echo_update_kernel(
                     out=dealt[:].rearrange("p (u e) c j -> p u c j e", e=2),
                     in_=raw.rearrange("p j c (u e) -> p u c j e", e=2),
                 )
-            elif engine == "scalar":
-                nc.scalar.copy(out=dealt[:].rearrange("p t c j -> p c j t"), in_=raw.rearrange("p j c t -> p c j t"))
             else:
-                nc.gpsimd.tensor_scalar(
-                    dealt[:].rearrange("p t c j -> p c t j"),
-                    raw.rearrange("p j c t -> p c t j"),
-                    1.0,
-                    0.0,
-                    ALU.mult,
-                    ALU.add,
-                )
+                nc.scalar.copy(out=dealt[:].rearrange("p t c j -> p c j t"), in_=raw.rearrange("p j c t -> p c j t"))
 
         def quantize_cor(b, g, on=None):
             cor_mx[b, g] = quantize(cor_bf[b, g][:].rearrange("p t c j -> p (t c j)"), f"cor{b}{g}", on)
@@ -261,7 +267,7 @@ def tile_list_subband_echo_update_kernel(
 
         def normalize_turned(blk):
             acc = bank(BLOCKS + blk)
-            for n, rows in enumerate((mic_sb[0], x[0])):
+            for n, rows in enumerate((mic_sb[0], x0)):
                 for i in range(PACK):
                     nc.tensor.matmul(
                         acc[:, turned_cols(i)],
@@ -318,30 +324,35 @@ def tile_list_subband_echo_update_kernel(
             inverse_root(root1[pair][:], pair_of(power_sb[1], pair))
         for pair in range(2):
             square(pair_of(power_sb[1], pair), root1[pair][:])
-        res1 = subtract(1, "tab1")
-        round_cor(0, 0, "gpsimd", "x1")
+        res1 = [subtract(nc.vector, 0, "tab1"), subtract(nc.gpsimd, 1, "x10")]
         for blk in range(BLOCKS):
             normalize_turned(blk)
         turn_back(0)
         turn_back(1)
         round_cor(0, 1, "scalar", "root03")
-        round_cor(1, 1, "scalar")
+        round_cor(0, 0, "vector", "x11")
+        round_cor(1, 0, "vector", "mic1")
         quantize_cor(0, 0, "h02")
-        z1 = normalize(1, res1, power_sb[1], None)
+        normalize(0, res1[0])
         z_mx = [quantize_z(0, z0, "h03")]
-        round_cor(1, 0, "vector", "tab1")
-        quantize_cor(0, 1, "h10")
-        z_mx.append(quantize_z(1, z1, "h11"))
+        normalize(1, res1[1])
         quantize_cor(1, 0, "h12")
+        z_mx.append(quantize_z(1, z1, "h11"))
+        quantize_cor(0, 1, "h10")
+        round_cor(1, 1, "scalar")
         quantize_cor(1, 1, "h13")
 
-        y = [prev_sb[0], tile([P, PACK, M], F32, "y1", "cor_bf11")]
-        for t in range(PACK):
-            nc.scalar.activation(
-                out=y[0][:, t, :], in_=prev_sb[0][:, t, :], func=ACT.Copy, scale=gain_sb[:, 0, t : t + 1]
-            )
-        for t in range(PACK):
-            nc.gpsimd.tensor_scalar(y[1][:, t, :], prev_sb[1][:, t, :], gain_sb[:, 1, t : t + 1], 0.0, ALU.mult, ALU.add)
+        scaled = {}
+        for t in range(SCALAR_ROWS):
+            row = tile([P, M], F32, f"scaled{t}")
+            scaled[0, t] = row[:]
+            nc.scalar.activation(out=row[:], in_=prev_sb[0][:, t, :], func=ACT.Copy, scale=gain_sb[:, 0, t : t + 1])
+        late = tile([P, 2 * PACK - SCALAR_ROWS, M], F32, "scaled_late", "cor_bf11")
+        for n in range(SCALAR_ROWS, 2 * PACK):
+            g, t = divmod(n, PACK)
+            scaled[g, t] = late[:, n - SCALAR_ROWS, :]
+            nc.gpsimd.tensor_scalar(scaled[g, t], prev_sb[g][:, t, :], gain_sb[:, g, t : t + 1], 0.0, ALU.mult, ALU.add)
+        y = [tile([P, PACK, M], F32, f"y{g}", f"power{g}") for g in range(2)]
 
         def product(acc, b, g, t):
             cols = slice(P * t, P * (t + 1))
@@ -362,13 +373,12 @@ def tile_list_subband_echo_update_kernel(
                 accs[g, t] = bank(2 + PACK * g + t)
                 product(accs[g, t], 0, g, t)
 
-        first_pass(0)
-        first_pass(1)
         for g in range(2):
+            first_pass(g)
             for t in range(PACK):
                 product(accs[g, t], 1, g, t)
                 nc.vector.scalar_tensor_tensor(
-                    y[g][:, t, :], accs[g, t][:], gain_sb[:, g, t : t + 1], y[g][:, t, :], ALU.mult, ALU.add
+                    y[g][:, t, :], accs[g, t][:], gain_sb[:, g, t : t + 1], scaled[g, t], ALU.mult, ALU.add
                 )
                 if t % 2:
                     nc.sync.dma_start(out=pair_of(group_rows(out_0, g), t // 2), in_=pair_of(y[g], t // 2))

@@ -63,10 +63,6 @@ def tile_list_subband_echo_update_kernel(
         nc.vector.memset(w4_sc[:].bitcast(I32), 0)
         v_sc = [tile([P, S], U8, f"v_sc{a}") for a in range(2)]
         nc.vector.memset(v_sc[1][:].bitcast(I32), 0)
-        one = tile([P, 1], F32, "one")
-        nc.vector.memset(one[:], 1.0)
-        warm = tile([P, 1], F32, "warm")
-        nc.scalar.activation(out=warm[:], in_=one[:], func=ACT.Abs_reciprocal_sqrt)
 
         ident = tile([P, P], F32, "ident")
         make_identity(nc, ident[:])

@@ -25,6 +25,7 @@ BANKS = 8
 BLOCKS = M // P
 EARLY_ROWS = 1
 AHEAD = 3
+H_BANKS = 2 * AHEAD
 HALF = M // 2
 SCALAR_ROWS = 4
 SCALAR_COLS = 256
@@ -149,7 +150,7 @@ def tile_list_subband_echo_update_kernel(
             words, scales = w4_dealt[b]
             cols = slice(BANK * half, BANK * (half + 1))
             if a == 0:
-                h_acc[b, i, half] = bank(EARLY_ROWS + 2 * (PACK * b + i) + half)
+                h_acc[b, i, half] = bank((2 * (PACK * b + i) + half) % H_BANKS)
             nc.tensor.matmul_mx(
                 out=h_acc[b, i, half][:],
                 lhsT=words[:, a, i, :].bitcast(FP4X4),
@@ -249,12 +250,16 @@ def tile_list_subband_echo_update_kernel(
 
         roots = {}
 
-        def turned_root(i):
-            acc = bank(i)
+        turned_power = {}
+
+        def turn_power(i, number):
+            turned_power[i] = bank(number)
             for blk in range(BLOCKS):
-                nc.tensor.transpose(acc[:, P * blk : P * (blk + 1)], block(power_sb[0], i, blk), ident[:])
+                nc.tensor.transpose(turned_power[i][:, P * blk : P * (blk + 1)], block(power_sb[0], i, blk), ident[:])
+
+        def turned_root(i):
             roots[i] = tile([P, BANK], F32, f"root0{i}")
-            inverse_root(roots[i][:], acc[:])
+            inverse_root(roots[i][:], turned_power[i][:])
 
         def square_turned(i):
             square(inverse0[:, :, turned_cols(i)], roots[i][:].rearrange("p (k c) -> p k c", k=BLOCKS))
@@ -262,7 +267,7 @@ def tile_list_subband_echo_update_kernel(
         z_turned = {}
 
         def normalize_turned(blk):
-            acc = bank(BLOCKS + blk)
+            acc = bank((H_BANKS - 1 + blk) % H_BANKS)
             for n, rows in enumerate((mic_sb[0], x0)):
                 for i in range(PACK):
                     nc.tensor.matmul(
@@ -284,7 +289,7 @@ def tile_list_subband_echo_update_kernel(
         z0 = tile([P, M, PACK], BF16, "z0", "v0")
 
         def turn_back(half):
-            acc = bank(half)
+            acc = bank(H_BANKS + half)
             for j in range(2):
                 words = z_turned[2 * half + j][:].bitcast(F32)
                 for u in range(2):
@@ -295,6 +300,7 @@ def tile_list_subband_echo_update_kernel(
                 in_=acc[:].rearrange("p (u c d) -> p c u d", u=2, d=2),
             )
 
+        turn_power(0, H_BANKS)
         turned_root(0)
         square_turned(0)
         for i in range(AHEAD):
@@ -306,11 +312,14 @@ def tile_list_subband_echo_update_kernel(
         for i in range(2, AHEAD):
             for half in range(2):
                 finish_half(0, i, half)
+        turn_power(1, H_BANKS + 1)
+        turn_power(2, H_BANKS)
         for b in range(2):
             for i in range(PACK):
                 if PACK * b + i >= AHEAD:
                     filter_rows(b, i)
                 pick(b, i)
+        turn_power(3, H_BANKS - 2)
         for i in range(EARLY_ROWS, PACK):
             turned_root(i)
         for i in range(1, PACK):
@@ -366,7 +375,7 @@ def tile_list_subband_echo_update_kernel(
 
         def first_pass(g):
             for t in range(PACK):
-                accs[g, t] = bank(2 + PACK * g + t)
+                accs[g, t] = bank(((3, 4, 5, 0), (1, 2, 6, 7))[g][t])
                 product(accs[g, t], 0, g, t)
 
         for g in range(2):

@@ -26,7 +26,7 @@ BLOCKS = M // P
 EARLY_ROWS = 1
 AHEAD = 3
 H_BANKS = 2 * AHEAD
-HALF = M // 2
+VECTOR_COLS = 288
 SCALAR_ROWS = 4
 SCALAR_COLS = 256
 RUN = 4
@@ -108,7 +108,7 @@ def tile_list_subband_echo_update_kernel(
         nc.sync.dma_start(out=power_sb[0][:, 1:PACK, :], in_=group_rows(power, 0)[:, 1:PACK, :])
         mic_sb = [load_group(mic, b, f"mic{b}") for b in range(2)]
         power_sb.append(load_group(power, 1, "power1"))
-        cor_raw = {(b, g): load_cor(b, g) for b in range(2) for g in range(2)}
+        cor_raw = {(b, g): load_cor(b, g) for g in range(2) for b in range(2)}
         gain_sb = tile([P, 2, PACK], F32, "gain_sb")
         nc.sync.dma_start(out=gain_sb[:], in_=gain.rearrange("(g p t) -> p g t", g=2, t=PACK))
         prev_sb = [load_group(prev, g, f"prev{g}") for g in range(2)]
@@ -178,23 +178,24 @@ def tile_list_subband_echo_update_kernel(
                 finish_half(b, i, half)
 
         x0 = tile([P, PACK, M], F32, "x0", "tab0")
-        x1 = [tile([P, PACK, HALF], F32, f"x1{half}") for half in range(2)]
+        parts = (slice(0, VECTOR_COLS), slice(VECTOR_COLS, M))
+        x1 = [tile([P, PACK, cols.stop - cols.start], F32, f"x1{half}") for half, cols in enumerate(parts)]
 
         def half_cols(half):
-            return slice(HALF * half, HALF * (half + 1))
+            return parts[half]
 
         def pick(b, i):
             if b == 0:
                 nc.vector.tensor_tensor(x0[:, i, :], h[b, i][:].indirect(idx2[:]), wgt_sb[:], ALU.mult)
             else:
                 for half in range(2):
-                    entries = idx2[:, HALF // 16 * half : HALF // 16 * (half + 1)]
+                    entries = idx2[:, parts[half].start // 16 : parts[half].stop // 16]
                     nc.vector.tensor_tensor(
                         x1[half][:, i, :], h[b, i][:].indirect(entries), wgt_sb[:, half_cols(half)], ALU.mult
                     )
 
         def subtract(engine, half, on):
-            res = tile([P, PACK, HALF], F32, f"res1{half}", on)
+            res = tile([P, PACK, parts[half].stop - parts[half].start], F32, f"res1{half}", on)
             engine.tensor_tensor(res[:], mic_sb[1][:, :, half_cols(half)], x1[half][:], ALU.subtract)
             return res
 
@@ -303,15 +304,15 @@ def tile_list_subband_echo_update_kernel(
         turn_power(0, H_BANKS)
         turned_root(0)
         square_turned(0)
-        for i in range(AHEAD):
-            for half in range(2):
-                filter_pass(0, 0, i, half)
-        for half in range(2):
-            for i in range(2):
-                finish_half(0, i, half)
-        for i in range(2, AHEAD):
-            for half in range(2):
-                finish_half(0, i, half)
+        filter_pass(0, 0, 0, 0)
+        filter_pass(0, 0, 1, 0)
+        filter_pass(0, 0, 0, 1)
+        finish_half(0, 0, 0)
+        finish_half(0, 1, 0)
+        filter_pass(0, 0, 1, 1)
+        finish_half(0, 0, 1)
+        finish_half(0, 1, 1)
+        filter_rows(0, 2)
         turn_power(1, H_BANKS + 1)
         turn_power(2, H_BANKS)
         for b in range(2):

@@ -27,6 +27,7 @@ EARLY_ROWS = 1
 AHEAD = 3
 H_BANKS = 2 * AHEAD
 VECTOR_COLS = 288
+VECTOR_COR = 32
 SCALAR_ROWS = 4
 SCALAR_COLS = 256
 RUN = 4
@@ -111,7 +112,10 @@ def tile_list_subband_echo_update_kernel(
         cor_raw = {(b, g): load_cor(b, g) for g in range(2) for b in range(2)}
         gain_sb = tile([P, 2, PACK], F32, "gain_sb")
         nc.sync.dma_start(out=gain_sb[:], in_=gain.rearrange("(g p t) -> p g t", g=2, t=PACK))
-        prev_sb = [load_group(prev, g, f"prev{g}") for g in range(2)]
+        prev_sb = [tile([P, PACK, M], F32, f"prev{g}") for g in range(2)]
+        for g, cuts in enumerate(((0, 2, 4), (0, 2, 3, 4))):
+            for first, last in zip(cuts, cuts[1:]):
+                nc.sync.dma_start(out=prev_sb[g][:, first:last, :], in_=group_rows(prev, g)[:, first:last, :])
 
         nc.vector.tensor_copy(v_sc[0][:], tab_sc[:].indirect(idx[:]))
         nc.scalar.dma_start(out=v_sc[1][0:112, :].bitcast(I32), in_=v_sc[0][16:128, :].bitcast(I32))
@@ -225,17 +229,18 @@ def tile_list_subband_echo_update_kernel(
         cor_bf = {}
         cor_mx = {}
 
-        def round_cor(b, g, engine, on=None):
-            dealt = tile([P, PACK, P, PACK], BF16, f"cor_bf{b}{g}", on)
-            cor_bf[b, g] = dealt
-            raw = cor_raw[b, g][:].rearrange("p j (c t) -> p j c t", t=PACK)
+        def round_cor(b, g, engine, on=None, cols=slice(0, P)):
+            if (b, g) not in cor_bf:
+                cor_bf[b, g] = tile([P, PACK, P, PACK], BF16, f"cor_bf{b}{g}", on)
+            dealt = cor_bf[b, g][:, :, cols, :]
+            raw = cor_raw[b, g][:].rearrange("p j (c t) -> p j c t", t=PACK)[:, :, cols, :]
             if engine == "vector":
                 nc.vector.tensor_copy(
-                    out=dealt[:].rearrange("p (u e) c j -> p u c j e", e=2),
+                    out=dealt.rearrange("p (u e) c j -> p u c j e", e=2),
                     in_=raw.rearrange("p j c (u e) -> p u c j e", e=2),
                 )
             else:
-                nc.scalar.copy(out=dealt[:].rearrange("p t c j -> p c j t"), in_=raw.rearrange("p j c t -> p c j t"))
+                nc.scalar.copy(out=dealt.rearrange("p t c j -> p c j t"), in_=raw.rearrange("p j c t -> p c j t"))
 
         def quantize_cor(b, g, on=None):
             cor_mx[b, g] = quantize(cor_bf[b, g][:].rearrange("p t c j -> p (t c j)"), f"cor{b}{g}", on)
@@ -344,8 +349,9 @@ def tile_list_subband_echo_update_kernel(
         normalize(1, res1[1])
         quantize_cor(1, 0, "h12")
         z_mx.append(quantize_z(1, z1, "h11"))
+        round_cor(1, 1, "scalar", None, slice(VECTOR_COR, P))
+        round_cor(1, 1, "vector", None, slice(0, VECTOR_COR))
         quantize_cor(0, 1, "h10")
-        round_cor(1, 1, "scalar")
         quantize_cor(1, 1, "h13")
 
         scaled = {}

@@ -97,6 +97,8 @@ def tile_list_subband_echo_update_kernel(
                 in_=w4_scales[:, 4 * q : 4 * q + 4, :].bitcast(I32).rearrange("a r c -> r a c"),
             )
         tab.append(load_table(1))
+        power_sb.append(tile([P, PACK, M], F32, "power1"))
+        nc.sync.dma_start(out=power_sb[1][:, 0, :], in_=group_rows(power, 1)[:, 0, :])
         w4_raw.append(load_w4(1))
         idx2 = lists.tile([P, M // 16], U16, name="idx2")
         nc.sync.dma_start(idx2[:], offs2)
@@ -108,7 +110,7 @@ def tile_list_subband_echo_update_kernel(
 
         nc.sync.dma_start(out=power_sb[0][:, 1:PACK, :], in_=group_rows(power, 0)[:, 1:PACK, :])
         mic_sb = [load_group(mic, b, f"mic{b}") for b in range(2)]
-        power_sb.append(load_group(power, 1, "power1"))
+        nc.sync.dma_start(out=power_sb[1][:, 1:PACK, :], in_=group_rows(power, 1)[:, 1:PACK, :])
         cor_raw = {(b, g): load_cor(b, g) for g in range(2) for b in range(2)}
         gain_sb = tile([P, 2, PACK], F32, "gain_sb")
         nc.sync.dma_start(out=gain_sb[:], in_=gain.rearrange("(g p t) -> p g t", g=2, t=PACK))
@@ -168,7 +170,7 @@ def tile_list_subband_echo_update_kernel(
         def finish_half(b, i, half):
             filter_pass(1, b, i, half)
             if half == 0:
-                h[b, i] = tile([P, S], F32, f"h{b}{i}")
+                h[b, i] = tile([P, S], F32, f"h{b}{i}", "root_early" if (b, i) == (0, 0) else None)
             nc.scalar.activation(
                 out=h[b, i][:, BANK * half : BANK * (half + 1)],
                 in_=h_acc[b, i, half][:],
@@ -309,6 +311,9 @@ def tile_list_subband_echo_update_kernel(
         turn_power(0, H_BANKS)
         turned_root(0)
         square_turned(0)
+        root_early = tile([P, M], F32, "root_early")
+        inverse_root(root_early[:], power_sb[1][:, 0, :])
+        square(power_sb[1][:, 0, :], root_early[:])
         filter_pass(0, 0, 0, 0)
         filter_pass(0, 0, 1, 0)
         filter_pass(0, 0, 0, 1)
@@ -330,11 +335,11 @@ def tile_list_subband_echo_update_kernel(
             turned_root(i)
         for i in range(1, PACK):
             square_turned(i)
-        root1 = [tile([P, 2, M], F32, f"root1{pair}", f"root0{2 + pair}") for pair in range(2)]
-        for pair in range(2):
-            inverse_root(root1[pair][:], pair_of(power_sb[1], pair))
-        for pair in range(2):
-            square(pair_of(power_sb[1], pair), root1[pair][:])
+        root1 = [tile([P, PACK - 1, cols.stop - cols.start], F32, f"root1{n}", f"root0{2 + n}") for n, cols in enumerate(parts)]
+        for root, cols in zip(root1, parts):
+            inverse_root(root[:], power_sb[1][:, 1:PACK, cols])
+        for root, cols in zip(root1, parts):
+            square(power_sb[1][:, 1:PACK, cols], root[:])
         res1 = [subtract(nc.vector, 0, "tab1"), subtract(nc.gpsimd, 1, "x10")]
         for blk in range(BLOCKS):
             normalize_turned(blk)
@@ -395,7 +400,7 @@ def tile_list_subband_echo_update_kernel(
                 if t % 2:
                     nc.sync.dma_start(out=pair_of(group_rows(out_0, g), t // 2), in_=pair_of(y[g], t // 2))
 
-        y_bf = [tile([P, M, PACK], BF16, f"y_bf{g}", f"h0{g}") for g in range(2)]
+        y_bf = [tile([P, M, PACK], BF16, f"y_bf{g}", ("root_early", "h01")[g]) for g in range(2)]
 
         def round_y(copy, g, cols):
             copy(out=words_by_pairs(y_bf[g][:, cols, :]), in_=by_pairs(y[g][:, :, cols]))

@@ -27,9 +27,8 @@ EARLY_ROWS = 1
 AHEAD = 3
 H_BANKS = 2 * AHEAD
 VECTOR_COLS = 288
-VECTOR_COR = 32
+VECTOR_COR = 96
 SCALAR_ROWS = 4
-SCALAR_COLS = 256
 RUN = 4
 
 
@@ -122,17 +121,17 @@ def tile_list_subband_echo_update_kernel(
         nc.vector.tensor_copy(v_sc[0][:], tab_sc[:].indirect(idx[:]))
         nc.scalar.dma_start(out=v_sc[1][0:112, :].bitcast(I32), in_=v_sc[0][16:128, :].bitcast(I32))
 
-        def deal_w4(b, words_on=None, scales_on=None):
+        def deal_w4(b, engine, scales_on=None):
             cols = slice(PASS * b, PASS * (b + 1))
-            words = tile([P, 2, PACK, 2 * P], U8, f"w4_dealt{b}", words_on)
+            words = tile([P, 2, PACK, 2 * P], U8, f"w4_dealt{b}")
             nc.vector.tensor_copy(
                 out=words[:].bitcast(U16), in_=w4_raw[b][:].bitcast(U16).rearrange("p a (c i) -> p a i c", i=PACK)
             )
             scales = tile([P, 2, PACK, P], U8, f"w4_sc_dealt{b}", scales_on)
-            nc.vector.tensor_copy(out=scales[:], in_=w4_sc[:, :, cols].rearrange("p a (c i) -> p a i c", i=PACK))
+            engine.tensor_copy(out=scales[:], in_=w4_sc[:, :, cols].rearrange("p a (c i) -> p a i c", i=PACK))
             return words, scales
 
-        w4_dealt = [deal_w4(0)]
+        w4_dealt = [deal_w4(0, nc.gpsimd)]
         v = [tile([P, S], U32, f"v{a}") for a in range(2)]
         nc.vector.tensor_copy(v[0][:], tab[0][:].bitcast(U32).indirect(idx[:]))
         for half in range(2):
@@ -140,7 +139,7 @@ def tile_list_subband_echo_update_kernel(
                 v[1][:, BANK * half : BANK * (half + 1)],
                 tab[1][:].bitcast(U32).indirect(idx[:, BANK // 16 * half : BANK // 16 * (half + 1)]),
             )
-        w4_dealt.append(deal_w4(1, None, "tab1"))
+        w4_dealt.append(deal_w4(1, nc.vector, "tab1"))
 
         def inverse_root(out, in_):
             nc.scalar.activation(out=out, in_=in_, func=ACT.Abs_reciprocal_sqrt)
@@ -345,17 +344,17 @@ def tile_list_subband_echo_update_kernel(
             normalize_turned(blk)
         turn_back(0)
         turn_back(1)
-        round_cor(0, 1, "scalar", "root03")
+        round_cor(1, 0, "scalar", "root03", slice(VECTOR_COR, P))
+        round_cor(0, 1, "scalar", "z_turned3")
         round_cor(0, 0, "vector", "x11")
-        round_cor(1, 0, "vector", "mic1")
+        round_cor(1, 0, "vector", None, slice(0, VECTOR_COR))
         quantize_cor(0, 0, "h02")
         normalize(0, res1[0])
         z_mx = [quantize_z(0, z0, "h03")]
         normalize(1, res1[1])
         quantize_cor(1, 0, "h12")
         z_mx.append(quantize_z(1, z1, "h11"))
-        round_cor(1, 1, "scalar", None, slice(VECTOR_COR, P))
-        round_cor(1, 1, "vector", None, slice(0, VECTOR_COR))
+        round_cor(1, 1, "scalar")
         quantize_cor(0, 1, "h10")
         quantize_cor(1, 1, "h13")
 
@@ -400,21 +399,24 @@ def tile_list_subband_echo_update_kernel(
                 if t % 2:
                     nc.sync.dma_start(out=pair_of(group_rows(out_0, g), t // 2), in_=pair_of(y[g], t // 2))
 
-        y_bf = [tile([P, M, PACK], BF16, f"y_bf{g}", ("root_early", "h01")[g]) for g in range(2)]
-
-        def round_y(copy, g, cols):
-            copy(out=words_by_pairs(y_bf[g][:, cols, :]), in_=by_pairs(y[g][:, :, cols]))
-
-        round_y(nc.scalar.copy, 0, slice(0, M))
-        round_y(nc.scalar.copy, 1, slice(0, SCALAR_COLS))
-        round_y(nc.vector.tensor_copy, 1, slice(SCALAR_COLS, M))
         y_sc = tile([P, 2, M], U8, "y_sc")
-        for g in range(2):
-            codes = tile([P, M], I32, f"y_codes{g}")
+
+        def round_y(copy, g, cols, on):
+            rounded = tile([P, cols.stop - cols.start, PACK], BF16, f"y_bf{g}{cols.start}", on)
+            copy(out=words_by_pairs(rounded[:]), in_=by_pairs(y[g][:, :, cols]))
+            return g, cols, rounded
+
+        pieces = [
+            round_y(nc.scalar.copy, 0, slice(0, M), "root_early"),
+            round_y(nc.vector.tensor_copy, 1, slice(M // 2, M), "h01"),
+            round_y(nc.scalar.copy, 1, slice(0, M // 2), None),
+        ]
+        for g, cols, rounded in pieces:
+            codes = tile([P, cols.stop - cols.start], I32, f"y_codes{g}{cols.start}")
             nc.vector.quantize_mx(
-                out=codes[:].bitcast(FP8X4), scales=y_sc[:, g, :], in_=y_bf[g][:].rearrange("p m t -> p (m t)")
+                out=codes[:].bitcast(FP8X4), scales=y_sc[:, g, cols], in_=rounded[:].rearrange("p m t -> p (m t)")
             )
-            nc.sync.dma_start(out=out_1[g].rearrange("p m t -> p (m t)").bitcast(I32), in_=codes[:])
+            nc.sync.dma_start(out=out_1[g].rearrange("p m t -> p (m t)").bitcast(I32)[:, cols], in_=codes[:])
         for q in range(4):
             queue = nc.scalar if q % 2 else nc.sync
             queue.dma_start(

@@ -121,17 +121,17 @@ def tile_list_subband_echo_update_kernel(
         nc.vector.tensor_copy(v_sc[0][:], tab_sc[:].indirect(idx[:]))
         nc.scalar.dma_start(out=v_sc[1][0:112, :].bitcast(I32), in_=v_sc[0][16:128, :].bitcast(I32))
 
-        def deal_w4(b, engine, scales_on=None):
+        def deal_w4(b, scales_on=None):
             cols = slice(PASS * b, PASS * (b + 1))
             words = tile([P, 2, PACK, 2 * P], U8, f"w4_dealt{b}")
             nc.vector.tensor_copy(
                 out=words[:].bitcast(U16), in_=w4_raw[b][:].bitcast(U16).rearrange("p a (c i) -> p a i c", i=PACK)
             )
             scales = tile([P, 2, PACK, P], U8, f"w4_sc_dealt{b}", scales_on)
-            engine.tensor_copy(out=scales[:], in_=w4_sc[:, :, cols].rearrange("p a (c i) -> p a i c", i=PACK))
+            nc.vector.tensor_copy(out=scales[:], in_=w4_sc[:, :, cols].rearrange("p a (c i) -> p a i c", i=PACK))
             return words, scales
 
-        w4_dealt = [deal_w4(0, nc.gpsimd)]
+        w4_dealt = [deal_w4(0)]
         v = [tile([P, S], U32, f"v{a}") for a in range(2)]
         nc.vector.tensor_copy(v[0][:], tab[0][:].bitcast(U32).indirect(idx[:]))
         for half in range(2):
@@ -139,7 +139,7 @@ def tile_list_subband_echo_update_kernel(
                 v[1][:, BANK * half : BANK * (half + 1)],
                 tab[1][:].bitcast(U32).indirect(idx[:, BANK // 16 * half : BANK // 16 * (half + 1)]),
             )
-        w4_dealt.append(deal_w4(1, nc.vector, "tab1"))
+        w4_dealt.append(deal_w4(1, "tab1"))
 
         def inverse_root(out, in_):
             nc.scalar.activation(out=out, in_=in_, func=ACT.Abs_reciprocal_sqrt)

@@ -23,12 +23,8 @@ PASS = P * PACK
 BANK = 512
 BANKS = 8
 BLOCKS = M // P
-EARLY_ROWS = 1
-AHEAD = 3
-H_BANKS = 2 * AHEAD
-VECTOR_COLS = 288
-VECTOR_COR = 96
-SCALAR_ROWS = 4
+H_BANKS = 6
+VECTOR_COR = 48
 RUN = 4
 
 
@@ -45,18 +41,13 @@ def tile_list_subband_echo_update_kernel(
             return sbuf.tile(shape, dtype, name=name, tag=on or name, align_bytes=64)
 
         def bank(number):
-            return psum.tile([P, BANK], F32, name="acc", tag=f"bank{number % BANKS}")
+            return psum.tile([P, BANK], F32, name="acc", tag=f"bank{number}")
 
         def group_rows(src, b):
             return src[PASS * b : PASS * (b + 1), :].rearrange("(p i) m -> p i m", i=PACK)
 
-        def load_group(src, b, name):
-            rows = tile([P, PACK, M], F32, name)
-            nc.sync.dma_start(out=rows[:], in_=group_rows(src, b))
-            return rows
-
-        def pair_of(rows, pair):
-            return rows[:, 2 * pair : 2 * pair + 2, :]
+        def load_rows(into, src, b, first, last):
+            nc.sync.dma_start(out=into, in_=group_rows(src, b)[:, first:last, :])
 
         tab_sc = tile([P, T], U8, "tab_sc")
         nc.gpsimd.memset(tab_sc[:].bitcast(I32), 0)
@@ -64,12 +55,11 @@ def tile_list_subband_echo_update_kernel(
         nc.vector.memset(w4_sc[:].bitcast(I32), 0)
         v_sc = [tile([P, S], U8, f"v_sc{a}") for a in range(2)]
         nc.vector.memset(v_sc[1][:].bitcast(I32), 0)
-
         ident = tile([P, P], F32, "ident")
         make_identity(nc, ident[:])
 
-        def load_w4(b):
-            words = tile([P, 2, PASS // 2], I32, f"w4_raw{b}")
+        def load_w4(b, on=None):
+            words = tile([P, 2, PASS // 2], I32, f"w4_raw{b}", on)
             cols = slice(PASS // 2 * b, PASS // 2 * (b + 1))
             nc.sync.dma_start(out=words[:], in_=w4_words.bitcast(I32)[:, :, cols].rearrange("a p c -> p a c"))
             return words
@@ -87,59 +77,50 @@ def tile_list_subband_echo_update_kernel(
             nc.sync.dma_start(out=words[:], in_=tab_words[a].rearrange("p t i -> p (t i)").bitcast(I32))
             return words
 
+        power_sb = [tile([P, PACK, M], F32, f"power{b}") for b in range(2)]
         tab = [load_table(0)]
-        power_sb = [tile([P, PACK, M], F32, "power0")]
-        nc.sync.dma_start(out=power_sb[0][:, 0, :], in_=group_rows(power, 0)[:, 0, :])
+        load_rows(power_sb[0][:, 0:1, :], power, 0, 0, 1)
         for q in range(4):
             nc.sync.dma_start(
                 out=w4_sc[32 * q : 32 * q + 4, :, :].bitcast(I32),
                 in_=w4_scales[:, 4 * q : 4 * q + 4, :].bitcast(I32).rearrange("a r c -> r a c"),
             )
+        load_rows(power_sb[1][:, 0:1, :], power, 1, 0, 1)
         tab.append(load_table(1))
-        power_sb.append(tile([P, PACK, M], F32, "power1"))
-        nc.sync.dma_start(out=power_sb[1][:, 0, :], in_=group_rows(power, 1)[:, 0, :])
-        w4_raw.append(load_w4(1))
+        load_rows(power_sb[1][:, 1:2, :], power, 1, 1, 2)
+        nc.vector.tensor_copy(v_sc[0][:], tab_sc[:].indirect(idx[:]))
+        nc.sync.dma_start(out=v_sc[1][0:112, :].bitcast(I32), in_=v_sc[0][16:128, :].bitcast(I32))
+        w4_raw.append(load_w4(1, "tab_sc"))
+
+        cor_raw = {}
+
+        def load_cor(b, g):
+            cor_raw[b, g] = tile([P, PACK, PASS], F32, f"cor{b}{g}")
+            load_rows(cor_raw[b, g][:], cor[:, PASS * g : PASS * (g + 1)], b, 0, PACK)
+
         idx2 = lists.tile([P, M // 16], U16, name="idx2")
         nc.sync.dma_start(idx2[:], offs2)
         wgt_sb = tile([P, M], F32, "wgt_sb")
         nc.sync.dma_start(out=wgt_sb[:], in_=wgt)
-
-        def load_cor(b, g):
-            return load_group(cor[:, PASS * g : PASS * (g + 1)], b, f"cor{b}{g}")
-
-        nc.sync.dma_start(out=power_sb[0][:, 1:PACK, :], in_=group_rows(power, 0)[:, 1:PACK, :])
-        mic_sb = [load_group(mic, b, f"mic{b}") for b in range(2)]
-        nc.sync.dma_start(out=power_sb[1][:, 1:PACK, :], in_=group_rows(power, 1)[:, 1:PACK, :])
-        cor_raw = {(b, g): load_cor(b, g) for g in range(2) for b in range(2)}
+        load_rows(power_sb[0][:, 1:PACK, :], power, 0, 1, PACK)
+        mic0 = tile([P, PACK, M], F32, "mic0")
+        load_rows(mic0[:], mic, 0, 0, PACK)
+        mic1_late = tile([P, 2, M], F32, "mic1_late")
+        load_rows(mic1_late[:], mic, 1, 2, PACK)
+        res1 = tile([P, PACK, M], F32, "res1")
+        load_rows(res1[:, 2:PACK, :], mic, 1, 0, 2)
+        load_rows(power_sb[1][:, 2:PACK, :], power, 1, 2, PACK)
+        load_cor(0, 0)
+        load_cor(1, 0)
+        load_cor(0, 1)
+        load_cor(1, 1)
         gain_sb = tile([P, 2, PACK], F32, "gain_sb")
         nc.sync.dma_start(out=gain_sb[:], in_=gain.rearrange("(g p t) -> p g t", g=2, t=PACK))
         prev_sb = [tile([P, PACK, M], F32, f"prev{g}") for g in range(2)]
         for g, cuts in enumerate(((0, 2, 4), (0, 2, 3, 4))):
             for first, last in zip(cuts, cuts[1:]):
-                nc.sync.dma_start(out=prev_sb[g][:, first:last, :], in_=group_rows(prev, g)[:, first:last, :])
+                load_rows(prev_sb[g][:, first:last, :], prev, g, first, last)
 
-        nc.vector.tensor_copy(v_sc[0][:], tab_sc[:].indirect(idx[:]))
-        nc.scalar.dma_start(out=v_sc[1][0:112, :].bitcast(I32), in_=v_sc[0][16:128, :].bitcast(I32))
-
-        def deal_w4(b, scales_on=None):
-            cols = slice(PASS * b, PASS * (b + 1))
-            words = tile([P, 2, PACK, 2 * P], U8, f"w4_dealt{b}")
-            nc.vector.tensor_copy(
-                out=words[:].bitcast(U16), in_=w4_raw[b][:].bitcast(U16).rearrange("p a (c i) -> p a i c", i=PACK)
-            )
-            scales = tile([P, 2, PACK, P], U8, f"w4_sc_dealt{b}", scales_on)
-            nc.vector.tensor_copy(out=scales[:], in_=w4_sc[:, :, cols].rearrange("p a (c i) -> p a i c", i=PACK))
-            return words, scales
-
-        w4_dealt = [deal_w4(0)]
-        v = [tile([P, S], U32, f"v{a}") for a in range(2)]
-        nc.vector.tensor_copy(v[0][:], tab[0][:].bitcast(U32).indirect(idx[:]))
-        for half in range(2):
-            nc.vector.tensor_copy(
-                v[1][:, BANK * half : BANK * (half + 1)],
-                tab[1][:].bitcast(U32).indirect(idx[:, BANK // 16 * half : BANK // 16 * (half + 1)]),
-            )
-        w4_dealt.append(deal_w4(1, "tab1"))
 
         def inverse_root(out, in_):
             nc.scalar.activation(out=out, in_=in_, func=ACT.Abs_reciprocal_sqrt)
@@ -147,88 +128,66 @@ def tile_list_subband_echo_update_kernel(
         def square(out, in_):
             nc.scalar.activation(out=out, in_=in_, func=ACT.Square)
 
-        h = {}
+        def deal_words(b, copy):
+            words = tile([P, 2, PACK, 2 * P], U8, f"w4_dealt{b}")
+            copy(out=words[:].bitcast(U16), in_=w4_raw[b][:].bitcast(U16).rearrange("p a (c i) -> p a i c", i=PACK))
+            return words
 
-        h_acc = {}
+        def deal_scales(b, on=None):
+            scales = tile([P, 2, PACK, P], U8, f"w4_sc_dealt{b}", on)
+            raw = w4_sc[:, :, PASS * b : PASS * (b + 1)]
+            nc.vector.tensor_copy(out=scales[:], in_=raw.rearrange("p a (c i) -> p a i c", i=PACK))
+            return scales
 
-        def filter_pass(a, b, i, half):
-            words, scales = w4_dealt[b]
-            cols = slice(BANK * half, BANK * (half + 1))
-            if a == 0:
-                h_acc[b, i, half] = bank((2 * (PACK * b + i) + half) % H_BANKS)
-            nc.tensor.matmul_mx(
-                out=h_acc[b, i, half][:],
-                lhsT=words[:, a, i, :].bitcast(FP4X4),
-                lhsT_scale=scales[:, a, i, :],
-                rhs=v[a][:, cols].bitcast(FP8X4),
-                rhs_scale=v_sc[a][:, cols],
-                start=(a == 0),
-                stop=(a == 1),
+        w4_dealt = [deal_words(0, nc.vector.tensor_copy)]
+
+        v = [tile([P, S], U32, f"v{a}") for a in range(2)]
+        nc.vector.tensor_copy(v[0][:], tab[0][:].bitcast(U32).indirect(idx[:]))
+        w4_sc_dealt = [deal_scales(0)]
+        for half in range(2):
+            nc.vector.tensor_copy(
+                v[1][:, BANK * half : BANK * (half + 1)],
+                tab[1][:].bitcast(U32).indirect(idx[:, BANK // 16 * half : BANK // 16 * (half + 1)]),
             )
+        w4_dealt.append(deal_words(1, nc.vector.tensor_copy))
+        w4_sc_dealt.append(deal_scales(1, "tab1"))
 
-        def finish_half(b, i, half):
-            filter_pass(1, b, i, half)
-            if half == 0:
-                h[b, i] = tile([P, S], F32, f"h{b}{i}", "root_early" if (b, i) == (0, 0) else None)
-            nc.scalar.activation(
-                out=h[b, i][:, BANK * half : BANK * (half + 1)],
-                in_=h_acc[b, i, half][:],
-                func=ACT.Copy,
-                scale=(-1.0, 1.0)[b],
-            )
+        def block(rows, i, blk):
+            return rows[:, i, P * blk : P * (blk + 1)]
 
-        def filter_rows(b, i):
-            for half in range(2):
-                filter_pass(0, b, i, half)
-                finish_half(b, i, half)
+        def turned_cols(i):
+            place = 2 * (i % 2) + i // 2
+            return slice(P * place, P * (place + 1))
 
-        x0 = tile([P, PACK, M], F32, "x0", "tab0")
-        parts = (slice(0, VECTOR_COLS), slice(VECTOR_COLS, M))
-        x1 = [tile([P, PACK, cols.stop - cols.start], F32, f"x1{half}") for half, cols in enumerate(parts)]
+        inverse0 = tile([P, BLOCKS, BANK], F32, "inverse0")
 
-        def half_cols(half):
-            return parts[half]
+        def turn_power(i, number):
+            acc = bank(number)
+            for blk in range(BLOCKS):
+                nc.tensor.transpose(acc[:, P * blk : P * (blk + 1)], block(power_sb[0], i, blk), ident[:])
+            return acc
 
-        def pick(b, i):
-            if b == 0:
-                nc.vector.tensor_tensor(x0[:, i, :], h[b, i][:].indirect(idx2[:]), wgt_sb[:], ALU.mult)
-            else:
-                for half in range(2):
-                    entries = idx2[:, parts[half].start // 16 : parts[half].stop // 16]
-                    nc.vector.tensor_tensor(
-                        x1[half][:, i, :], h[b, i][:].indirect(entries), wgt_sb[:, half_cols(half)], ALU.mult
-                    )
+        def invert_turned(rows, turned):
+            roots = [tile([P, BANK], F32, f"root0{i}") for i in rows]
+            for root, acc in zip(roots, turned):
+                inverse_root(root[:], acc[:])
+            for root, i in zip(roots, rows):
+                square(inverse0[:, :, turned_cols(i)], root[:].rearrange("p (k c) -> p k c", k=BLOCKS))
 
-        def subtract(engine, half, on):
-            res = tile([P, PACK, parts[half].stop - parts[half].start], F32, f"res1{half}", on)
-            engine.tensor_tensor(res[:], mic_sb[1][:, :, half_cols(half)], x1[half][:], ALU.subtract)
-            return res
+        invert_turned((0,), [turn_power(0, H_BANKS)])
+        for i in range(2):
+            root_early = tile([P, M], F32, f"root_early{i}")
+            inverse_root(root_early[:], power_sb[1][:, i, :])
+            square(power_sb[1][:, i, :], root_early[:])
 
-        def by_pairs(rows):
-            return rows.rearrange("p i (c e) -> p c i e", e=RUN)
-
-        def words_by_pairs(words):
-            return words.rearrange("p (c e) i -> p c i e", e=RUN)
-
-        z1 = tile([P, M, PACK], BF16, "z1")
-
-        def normalize(half, res):
-            cols = half_cols(half)
-            nc.vector.tensor_tensor(
-                words_by_pairs(z1[:, cols, :]), by_pairs(res[:]), by_pairs(power_sb[1][:, :, cols]), ALU.mult
-            )
+        cor_bf = {}
+        cor_mx = {}
 
         def quantize(values, name, on=None):
             codes = tile([P, BANK], U32, f"{name}_codes", on)
             scales = tile([P, BANK], U8, f"{name}_sc")
             nc.vector.quantize_mx(out=codes[:].bitcast(FP8X4), scales=scales[:], in_=values)
             return codes, scales
-
-        def quantize_z(b, z, on):
-            return quantize(z[:].rearrange("p m i -> p (m i)"), f"z{b}", on)
-
-        cor_bf = {}
-        cor_mx = {}
 
         def round_cor(b, g, engine, on=None, cols=slice(0, P)):
             if (b, g) not in cor_bf:
@@ -246,36 +205,77 @@ def tile_list_subband_echo_update_kernel(
         def quantize_cor(b, g, on=None):
             cor_mx[b, g] = quantize(cor_bf[b, g][:].rearrange("p t c j -> p (t c j)"), f"cor{b}{g}", on)
 
-        def turned_cols(i):
-            place = 2 * (i % 2) + i // 2
-            return slice(P * place, P * (place + 1))
+        h = {}
+        h_acc = {}
 
-        def block(rows, i, blk):
-            return rows[:, i, P * blk : P * (blk + 1)]
+        def filter_pass(a, b, i, half):
+            cols = slice(BANK * half, BANK * (half + 1))
+            if a == 0:
+                h_acc[b, i, half] = bank((2 * (PACK * b + i) + half) % H_BANKS)
+            nc.tensor.matmul_mx(
+                out=h_acc[b, i, half][:],
+                lhsT=w4_dealt[b][:, a, i, :].bitcast(FP4X4),
+                lhsT_scale=w4_sc_dealt[b][:, a, i, :],
+                rhs=v[a][:, cols].bitcast(FP8X4),
+                rhs_scale=v_sc[a][:, cols],
+                start=(a == 0),
+                stop=(a == 1),
+            )
 
-        inverse0 = tile([P, BLOCKS, BANK], F32, "inverse0")
+        def finish_half(b, i, half):
+            filter_pass(1, b, i, half)
+            if half == 0:
+                h[b, i] = tile([P, S], F32, f"h{b}{i}", "root_early1" if (b, i) == (0, 0) else None)
+            nc.scalar.activation(
+                out=h[b, i][:, BANK * half : BANK * (half + 1)],
+                in_=h_acc[b, i, half][:],
+                func=ACT.Copy,
+                scale=(-1.0, 1.0)[b],
+            )
 
-        roots = {}
+        def filter_rows(b, i):
+            for half in range(2):
+                filter_pass(0, b, i, half)
+                finish_half(b, i, half)
 
-        turned_power = {}
+        x = [tile([P, PACK, M], F32, f"x{b}", ("tab0", None)[b]) for b in range(2)]
 
-        def turn_power(i, number):
-            turned_power[i] = bank(number)
-            for blk in range(BLOCKS):
-                nc.tensor.transpose(turned_power[i][:, P * blk : P * (blk + 1)], block(power_sb[0], i, blk), ident[:])
+        def pick(b, i):
+            nc.vector.tensor_tensor(x[b][:, i, :], h[b, i][:].indirect(idx2[:]), wgt_sb[:], ALU.mult)
 
-        def turned_root(i):
-            roots[i] = tile([P, BANK], F32, f"root0{i}")
-            inverse_root(roots[i][:], turned_power[i][:])
+        filter_pass(0, 0, 0, 0)
+        filter_pass(0, 0, 1, 0)
+        filter_pass(0, 0, 0, 1)
+        finish_half(0, 0, 0)
+        finish_half(0, 1, 0)
+        filter_pass(0, 0, 1, 1)
+        finish_half(0, 0, 1)
+        finish_half(0, 1, 1)
+        filter_rows(0, 2)
+        turned_late = [turn_power(1, H_BANKS + 1), turn_power(2, H_BANKS)]
+        for b in range(2):
+            for i in range(PACK):
+                if PACK * b + i >= H_BANKS // 2:
+                    filter_rows(b, i)
+                pick(b, i)
+        turned_late.append(turn_power(3, H_BANKS - 2))
 
-        def square_turned(i):
-            square(inverse0[:, :, turned_cols(i)], roots[i][:].rearrange("p (k c) -> p k c", k=BLOCKS))
+        invert_turned((1, 2, 3), turned_late)
+        halves = (slice(0, M // 2), slice(M // 2, M))
+        root1 = [tile([P, M], F32, f"root1{i}", f"root0{i}") for i in (2, 3)]
+        for root, i in zip(root1, (2, 3)):
+            inverse_root(root[:], power_sb[1][:, i, :])
+        for root, i in zip(root1, (2, 3)):
+            square(power_sb[1][:, i, :], root[:])
+
+        nc.vector.tensor_tensor(res1[:, 0:2, :], res1[:, 2:PACK, :], x[1][:, 0:2, :], ALU.subtract)
+        nc.gpsimd.tensor_tensor(res1[:, 2:PACK, :], mic1_late[:], x[1][:, 2:PACK, :], ALU.subtract)
 
         z_turned = {}
 
         def normalize_turned(blk):
             acc = bank((H_BANKS - 1 + blk) % H_BANKS)
-            for n, rows in enumerate((mic_sb[0], x0)):
+            for n, rows in enumerate((mic0, x[0])):
                 for i in range(PACK):
                     nc.tensor.matmul(
                         acc[:, turned_cols(i)],
@@ -293,6 +293,9 @@ def tile_list_subband_echo_update_kernel(
                 ALU.mult,
             )
 
+        for blk in range(BLOCKS):
+            normalize_turned(blk)
+
         z0 = tile([P, M, PACK], BF16, "z0", "v0")
 
         def turn_back(half):
@@ -307,51 +310,32 @@ def tile_list_subband_echo_update_kernel(
                 in_=acc[:].rearrange("p (u c d) -> p c u d", u=2, d=2),
             )
 
-        turn_power(0, H_BANKS)
-        turned_root(0)
-        square_turned(0)
-        root_early = tile([P, M], F32, "root_early")
-        inverse_root(root_early[:], power_sb[1][:, 0, :])
-        square(power_sb[1][:, 0, :], root_early[:])
-        filter_pass(0, 0, 0, 0)
-        filter_pass(0, 0, 1, 0)
-        filter_pass(0, 0, 0, 1)
-        finish_half(0, 0, 0)
-        finish_half(0, 1, 0)
-        filter_pass(0, 0, 1, 1)
-        finish_half(0, 0, 1)
-        finish_half(0, 1, 1)
-        filter_rows(0, 2)
-        turn_power(1, H_BANKS + 1)
-        turn_power(2, H_BANKS)
-        for b in range(2):
-            for i in range(PACK):
-                if PACK * b + i >= AHEAD:
-                    filter_rows(b, i)
-                pick(b, i)
-        turn_power(3, H_BANKS - 2)
-        for i in range(EARLY_ROWS, PACK):
-            turned_root(i)
-        for i in range(1, PACK):
-            square_turned(i)
-        root1 = [tile([P, PACK - 1, cols.stop - cols.start], F32, f"root1{n}", f"root0{2 + n}") for n, cols in enumerate(parts)]
-        for root, cols in zip(root1, parts):
-            inverse_root(root[:], power_sb[1][:, 1:PACK, cols])
-        for root, cols in zip(root1, parts):
-            square(power_sb[1][:, 1:PACK, cols], root[:])
-        res1 = [subtract(nc.vector, 0, "tab1"), subtract(nc.gpsimd, 1, "x10")]
-        for blk in range(BLOCKS):
-            normalize_turned(blk)
+        def by_runs(rows):
+            return rows.rearrange("p i (c e) -> p c i e", e=RUN)
+
+        def words_by_runs(words):
+            return words.rearrange("p (c e) i -> p c i e", e=RUN)
+
+        z1 = tile([P, M, PACK], BF16, "z1")
+
+        def normalize(cols):
+            nc.vector.tensor_tensor(
+                words_by_runs(z1[:, cols, :]), by_runs(res1[:, :, cols]), by_runs(power_sb[1][:, :, cols]), ALU.mult
+            )
+
+        def quantize_z(b, z, on):
+            return quantize(z[:].rearrange("p m i -> p (m i)"), f"z{b}", on)
+
+        round_cor(1, 0, "scalar", "root03", slice(VECTOR_COR, P))
         turn_back(0)
         turn_back(1)
-        round_cor(1, 0, "scalar", "root03", slice(VECTOR_COR, P))
         round_cor(0, 1, "scalar", "z_turned3")
-        round_cor(0, 0, "vector", "x11")
+        round_cor(0, 0, "vector", "mic1_late")
         round_cor(1, 0, "vector", None, slice(0, VECTOR_COR))
         quantize_cor(0, 0, "h02")
-        normalize(0, res1[0])
+        normalize(halves[0])
         z_mx = [quantize_z(0, z0, "h03")]
-        normalize(1, res1[1])
+        normalize(halves[1])
         quantize_cor(1, 0, "h12")
         z_mx.append(quantize_z(1, z1, "h11"))
         round_cor(1, 1, "scalar")
@@ -359,15 +343,14 @@ def tile_list_subband_echo_update_kernel(
         quantize_cor(1, 1, "h13")
 
         scaled = {}
-        for t in range(SCALAR_ROWS):
+        for t in range(PACK):
             row = tile([P, M], F32, f"scaled{t}")
             scaled[0, t] = row[:]
             nc.scalar.activation(out=row[:], in_=prev_sb[0][:, t, :], func=ACT.Copy, scale=gain_sb[:, 0, t : t + 1])
-        late = tile([P, 2 * PACK - SCALAR_ROWS, M], F32, "scaled_late", "cor_bf11")
-        for n in range(SCALAR_ROWS, 2 * PACK):
-            g, t = divmod(n, PACK)
-            scaled[g, t] = late[:, n - SCALAR_ROWS, :]
-            nc.gpsimd.tensor_scalar(scaled[g, t], prev_sb[g][:, t, :], gain_sb[:, g, t : t + 1], 0.0, ALU.mult, ALU.add)
+        late = tile([P, PACK, M], F32, "scaled_late", "cor_bf11")
+        for t in range(PACK):
+            scaled[1, t] = late[:, t, :]
+            nc.gpsimd.tensor_scalar(scaled[1, t], prev_sb[1][:, t, :], gain_sb[:, 1, t : t + 1], 0.0, ALU.mult, ALU.add)
         y = [tile([P, PACK, M], F32, f"y{g}", f"power{g}") for g in range(2)]
 
         def product(acc, b, g, t):
@@ -382,34 +365,29 @@ def tile_list_subband_echo_update_kernel(
                 stop=(b == 1),
             )
 
-        accs = {}
-
-        def first_pass(g):
-            for t in range(PACK):
-                accs[g, t] = bank(((3, 4, 5, 0), (1, 2, 6, 7))[g][t])
-                product(accs[g, t], 0, g, t)
-
         for g in range(2):
-            first_pass(g)
+            accs = [bank(number) for number in ((3, 4, 5, 0), (1, 2, 6, 7))[g]]
             for t in range(PACK):
-                product(accs[g, t], 1, g, t)
+                product(accs[t], 0, g, t)
+            for t in range(PACK):
+                product(accs[t], 1, g, t)
                 nc.vector.scalar_tensor_tensor(
-                    y[g][:, t, :], accs[g, t][:], gain_sb[:, g, t : t + 1], scaled[g, t], ALU.mult, ALU.add
+                    y[g][:, t, :], accs[t][:], gain_sb[:, g, t : t + 1], scaled[g, t], ALU.mult, ALU.add
                 )
                 if t % 2:
-                    nc.sync.dma_start(out=pair_of(group_rows(out_0, g), t // 2), in_=pair_of(y[g], t // 2))
+                    nc.sync.dma_start(out=group_rows(out_0, g)[:, t - 1 : t + 1, :], in_=y[g][:, t - 1 : t + 1, :])
 
         y_sc = tile([P, 2, M], U8, "y_sc")
 
         def round_y(copy, g, cols, on):
             rounded = tile([P, cols.stop - cols.start, PACK], BF16, f"y_bf{g}{cols.start}", on)
-            copy(out=words_by_pairs(rounded[:]), in_=by_pairs(y[g][:, :, cols]))
+            copy(out=words_by_runs(rounded[:]), in_=by_runs(y[g][:, :, cols]))
             return g, cols, rounded
 
         pieces = [
-            round_y(nc.scalar.copy, 0, slice(0, M), "root_early"),
-            round_y(nc.vector.tensor_copy, 1, slice(M // 2, M), "h01"),
-            round_y(nc.scalar.copy, 1, slice(0, M // 2), None),
+            round_y(nc.scalar.copy, 0, slice(0, M), "root_early1"),
+            round_y(nc.vector.tensor_copy, 1, halves[1], "h01"),
+            round_y(nc.scalar.copy, 1, halves[0], None),
         ]
         for g, cols, rounded in pieces:
             codes = tile([P, cols.stop - cols.start], I32, f"y_codes{g}{cols.start}")

@@ -24,7 +24,7 @@ BANK = 512
 BANKS = 8
 BLOCKS = M // P
 H_BANKS = 6
-VECTOR_COR = 48
+VECTOR_COR = 64
 RUN = 4
 
 
@@ -110,8 +110,8 @@ def tile_list_subband_echo_update_kernel(
         res1 = tile([P, PACK, M], F32, "res1")
         load_rows(res1[:, 2:PACK, :], mic, 1, 0, 2)
         load_rows(power_sb[1][:, 2:PACK, :], power, 1, 2, PACK)
-        load_cor(0, 0)
         load_cor(1, 0)
+        load_cor(0, 0)
         load_cor(0, 1)
         load_cor(1, 1)
         gain_sb = tile([P, 2, PACK], F32, "gain_sb")
@@ -144,10 +144,10 @@ def tile_list_subband_echo_update_kernel(
         v = [tile([P, S], U32, f"v{a}") for a in range(2)]
         nc.vector.tensor_copy(v[0][:], tab[0][:].bitcast(U32).indirect(idx[:]))
         w4_sc_dealt = [deal_scales(0)]
-        for half in range(2):
+        quarters = (slice(BANK, BANK + BANK // 2), slice(BANK + BANK // 2, S))
+        for cols in (slice(0, BANK),) + quarters:
             nc.vector.tensor_copy(
-                v[1][:, BANK * half : BANK * (half + 1)],
-                tab[1][:].bitcast(U32).indirect(idx[:, BANK // 16 * half : BANK // 16 * (half + 1)]),
+                v[1][:, cols], tab[1][:].bitcast(U32).indirect(idx[:, cols.start // 16 : cols.stop // 16])
             )
         w4_dealt.append(deal_words(1, nc.vector.tensor_copy))
         w4_sc_dealt.append(deal_scales(1, "tab1"))
@@ -167,14 +167,13 @@ def tile_list_subband_echo_update_kernel(
                 nc.tensor.transpose(acc[:, P * blk : P * (blk + 1)], block(power_sb[0], i, blk), ident[:])
             return acc
 
-        def invert_turned(rows, turned):
-            roots = [tile([P, BANK], F32, f"root0{i}") for i in rows]
-            for root, acc in zip(roots, turned):
-                inverse_root(root[:], acc[:])
-            for root, i in zip(roots, rows):
-                square(inverse0[:, :, turned_cols(i)], root[:].rearrange("p (k c) -> p k c", k=BLOCKS))
+        roots0 = tile([P, BLOCKS, BANK], F32, "roots0")
 
-        invert_turned((0,), [turn_power(0, H_BANKS)])
+        def turned_root(i, acc):
+            inverse_root(roots0[:, :, turned_cols(i)], acc[:].rearrange("p (k c) -> p k c", k=BLOCKS))
+
+        turned_root(0, turn_power(0, H_BANKS))
+        square(inverse0[:, :, 0:P], roots0[:, :, 0:P])
         for i in range(2):
             root_early = tile([P, M], F32, f"root_early{i}")
             inverse_root(root_early[:], power_sb[1][:, i, :])
@@ -208,12 +207,16 @@ def tile_list_subband_echo_update_kernel(
         h = {}
         h_acc = {}
 
-        def filter_pass(a, b, i, half):
-            cols = slice(BANK * half, BANK * (half + 1))
+        def half_cols(half):
+            return slice(BANK * half, BANK * (half + 1))
+
+        def filter_pass(a, b, i, cols, number=None):
             if a == 0:
-                h_acc[b, i, half] = bank((2 * (PACK * b + i) + half) % H_BANKS)
+                if number is None:
+                    number = (2 * (PACK * b + i) + cols.start // BANK) % H_BANKS
+                h_acc[b, i, cols.start] = bank(number)[:, 0 : cols.stop - cols.start]
             nc.tensor.matmul_mx(
-                out=h_acc[b, i, half][:],
+                out=h_acc[b, i, cols.start],
                 lhsT=w4_dealt[b][:, a, i, :].bitcast(FP4X4),
                 lhsT_scale=w4_sc_dealt[b][:, a, i, :],
                 rhs=v[a][:, cols].bitcast(FP8X4),
@@ -222,35 +225,37 @@ def tile_list_subband_echo_update_kernel(
                 stop=(a == 1),
             )
 
-        def finish_half(b, i, half):
-            filter_pass(1, b, i, half)
-            if half == 0:
+        def finish(b, i, cols):
+            filter_pass(1, b, i, cols)
+            if cols.start == 0:
                 h[b, i] = tile([P, S], F32, f"h{b}{i}", "root_early1" if (b, i) == (0, 0) else None)
             nc.scalar.activation(
-                out=h[b, i][:, BANK * half : BANK * (half + 1)],
-                in_=h_acc[b, i, half][:],
+                out=h[b, i][:, cols],
+                in_=h_acc[b, i, cols.start],
                 func=ACT.Copy,
                 scale=(-1.0, 1.0)[b],
             )
 
         def filter_rows(b, i):
             for half in range(2):
-                filter_pass(0, b, i, half)
-                finish_half(b, i, half)
+                filter_pass(0, b, i, half_cols(half))
+                finish(b, i, half_cols(half))
 
         x = [tile([P, PACK, M], F32, f"x{b}", ("tab0", None)[b]) for b in range(2)]
 
         def pick(b, i):
             nc.vector.tensor_tensor(x[b][:, i, :], h[b, i][:].indirect(idx2[:]), wgt_sb[:], ALU.mult)
 
-        filter_pass(0, 0, 0, 0)
-        filter_pass(0, 0, 1, 0)
-        filter_pass(0, 0, 0, 1)
-        finish_half(0, 0, 0)
-        finish_half(0, 1, 0)
-        filter_pass(0, 0, 1, 1)
-        finish_half(0, 0, 1)
-        finish_half(0, 1, 1)
+        filter_pass(0, 0, 0, half_cols(0))
+        filter_pass(0, 0, 1, half_cols(0))
+        filter_pass(0, 0, 0, quarters[0])
+        filter_pass(0, 0, 0, quarters[1], H_BANKS + 1)
+        finish(0, 0, half_cols(0))
+        finish(0, 1, half_cols(0))
+        filter_pass(0, 0, 1, half_cols(1))
+        finish(0, 0, quarters[0])
+        finish(0, 0, quarters[1])
+        finish(0, 1, half_cols(1))
         filter_rows(0, 2)
         turned_late = [turn_power(1, H_BANKS + 1), turn_power(2, H_BANKS)]
         for b in range(2):
@@ -260,9 +265,12 @@ def tile_list_subband_echo_update_kernel(
                 pick(b, i)
         turned_late.append(turn_power(3, H_BANKS - 2))
 
-        invert_turned((1, 2, 3), turned_late)
+        for i, acc in enumerate(turned_late):
+            turned_root(1 + i, acc)
+        for blks, cols in ((slice(0, 2), slice(P, 3 * P)), (slice(0, 2), slice(3 * P, BANK)), (slice(2, BLOCKS), slice(P, BANK))):
+            square(inverse0[:, blks, cols], roots0[:, blks, cols])
         halves = (slice(0, M // 2), slice(M // 2, M))
-        root1 = [tile([P, M], F32, f"root1{i}", f"root0{i}") for i in (2, 3)]
+        root1 = [tile([P, M], F32, f"root1{i}", on) for i, on in ((2, "h12"), (3, "h11"))]
         for root, i in zip(root1, (2, 3)):
             inverse_root(root[:], power_sb[1][:, i, :])
         for root, i in zip(root1, (2, 3)):
@@ -318,26 +326,20 @@ def tile_list_subband_echo_update_kernel(
 
         z1 = tile([P, M, PACK], BF16, "z1")
 
-        def normalize(cols):
-            nc.vector.tensor_tensor(
-                words_by_runs(z1[:, cols, :]), by_runs(res1[:, :, cols]), by_runs(power_sb[1][:, :, cols]), ALU.mult
-            )
-
         def quantize_z(b, z, on):
             return quantize(z[:].rearrange("p m i -> p (m i)"), f"z{b}", on)
 
-        round_cor(1, 0, "scalar", "root03", slice(VECTOR_COR, P))
+        round_cor(1, 0, "scalar", "h12", slice(VECTOR_COR, P))
         turn_back(0)
         turn_back(1)
         round_cor(0, 1, "scalar", "z_turned3")
-        round_cor(0, 0, "vector", "mic1_late")
         round_cor(1, 0, "vector", None, slice(0, VECTOR_COR))
+        nc.vector.tensor_tensor(words_by_runs(z1[:]), by_runs(res1[:]), by_runs(power_sb[1][:]), ALU.mult)
+        quantize_cor(1, 0, "h01")
+        z_mx = {1: quantize_z(1, z1, "h11")}
+        round_cor(0, 0, "vector", "res1")
+        z_mx[0] = quantize_z(0, z0, "h03")
         quantize_cor(0, 0, "h02")
-        normalize(halves[0])
-        z_mx = [quantize_z(0, z0, "h03")]
-        normalize(halves[1])
-        quantize_cor(1, 0, "h12")
-        z_mx.append(quantize_z(1, z1, "h11"))
         round_cor(1, 1, "scalar")
         quantize_cor(0, 1, "h10")
         quantize_cor(1, 1, "h13")
@@ -361,16 +363,16 @@ def tile_list_subband_echo_update_kernel(
                 lhsT_scale=cor_mx[b, g][1][:, cols],
                 rhs=z_mx[b][0][:].bitcast(FP8X4),
                 rhs_scale=z_mx[b][1][:],
-                start=(b == 0),
-                stop=(b == 1),
+                start=(b != g),
+                stop=(b == g),
             )
 
         for g in range(2):
             accs = [bank(number) for number in ((3, 4, 5, 0), (1, 2, 6, 7))[g]]
             for t in range(PACK):
-                product(accs[t], 0, g, t)
+                product(accs[t], 1 - g, g, t)
             for t in range(PACK):
-                product(accs[t], 1, g, t)
+                product(accs[t], g, g, t)
                 nc.vector.scalar_tensor_tensor(
                     y[g][:, t, :], accs[t][:], gain_sb[:, g, t : t + 1], scaled[g, t], ALU.mult, ALU.add
                 )

@@ -247,14 +247,14 @@ def tile_list_subband_echo_update_kernel(
             nc.vector.tensor_tensor(x[b][:, i, :], h[b, i][:].indirect(idx2[:]), wgt_sb[:], ALU.mult)
 
         filter_pass(0, 0, 0, half_cols(0))
-        filter_pass(0, 0, 1, half_cols(0))
         filter_pass(0, 0, 0, quarters[0])
         filter_pass(0, 0, 0, quarters[1], H_BANKS + 1)
         finish(0, 0, half_cols(0))
-        finish(0, 1, half_cols(0))
-        filter_pass(0, 0, 1, half_cols(1))
+        filter_pass(0, 0, 1, half_cols(0))
         finish(0, 0, quarters[0])
         finish(0, 0, quarters[1])
+        finish(0, 1, half_cols(0))
+        filter_pass(0, 0, 1, half_cols(1))
         finish(0, 1, half_cols(1))
         filter_rows(0, 2)
         turned_late = [turn_power(1, H_BANKS + 1), turn_power(2, H_BANKS)]

@@ -133,8 +133,8 @@ def tile_list_subband_echo_update_kernel(
             copy(out=words[:].bitcast(U16), in_=w4_raw[b][:].bitcast(U16).rearrange("p a (c i) -> p a i c", i=PACK))
             return words
 
-        def deal_scales(b, on=None):
-            scales = tile([P, 2, PACK, P], U8, f"w4_sc_dealt{b}", on)
+        def deal_scales(b):
+            scales = tile([P, 2, PACK, P], U8, f"w4_sc_dealt{b}")
             raw = w4_sc[:, :, PASS * b : PASS * (b + 1)]
             nc.vector.tensor_copy(out=scales[:], in_=raw.rearrange("p a (c i) -> p a i c", i=PACK))
             return scales
@@ -143,14 +143,13 @@ def tile_list_subband_echo_update_kernel(
 
         v = [tile([P, S], U32, f"v{a}") for a in range(2)]
         nc.vector.tensor_copy(v[0][:], tab[0][:].bitcast(U32).indirect(idx[:]))
-        w4_sc_dealt = [deal_scales(0)]
+        w4_sc_dealt = [deal_scales(b) for b in range(2)]
         quarters = (slice(BANK, BANK + BANK // 2), slice(BANK + BANK // 2, S))
         for cols in (slice(0, BANK),) + quarters:
             nc.vector.tensor_copy(
                 v[1][:, cols], tab[1][:].bitcast(U32).indirect(idx[:, cols.start // 16 : cols.stop // 16])
             )
         w4_dealt.append(deal_words(1, nc.vector.tensor_copy))
-        w4_sc_dealt.append(deal_scales(1, "tab1"))
 
         def block(rows, i, blk):
             return rows[:, i, P * blk : P * (blk + 1)]

from contextlib import ExitStack

import concourse.mybir as mybir
from concourse.masks import make_identity

K, T, S, M, H, N = 1024, 2048, 1024, 512, 1024, 1024
FLOPS = 2 * K * H * S + 2 * H * N * M

F32 = mybir.dt.float32
BF16 = mybir.dt.bfloat16
I32 = mybir.dt.int32
U32 = mybir.dt.uint32
U16 = mybir.dt.uint16
U8 = mybir.dt.uint8
FP8X4 = mybir.dt.float8_e4m3fn_x4
FP4X4 = mybir.dt.float4_e2m1fn_x4
ACT = mybir.ActivationFunctionType
ALU = mybir.AluOpType

P = 128
PACK = 4
PASS = P * PACK
BANK = 512
BANKS = 8
BLOCKS = M // P
H_BANKS = 6
VECTOR_COR = 64
RUN = 4


def tile_list_subband_echo_update_kernel(
    tc, tab_words, tab_scales, offs, offs2, wgt, w4_words, w4_scales, mic, power, cor, prev, gain, out_0, out_1, out_2
):
    nc = tc.nc
    with ExitStack() as ctx:
        lists = ctx.enter_context(tc.tile_pool(name="lists", bufs=1))
        sbuf = ctx.enter_context(tc.tile_pool(name="sbuf", bufs=1))
        psum = ctx.enter_context(tc.psum_pool(name="psum", bufs=1))

        def tile(shape, dtype, name, on=None):
            return sbuf.tile(shape, dtype, name=name, tag=on or name, align_bytes=64)

        def bank(number):
            return psum.tile([P, BANK], F32, name="acc", tag=f"bank{number}")

        def group_rows(src, b):
            return src[PASS * b : PASS * (b + 1), :].rearrange("(p i) m -> p i m", i=PACK)

        def load_rows(into, src, b, first, last):
            nc.sync.dma_start(out=into, in_=group_rows(src, b)[:, first:last, :])

        tab_sc = tile([P, T], U8, "tab_sc")
        nc.gpsimd.memset(tab_sc[:].bitcast(I32), 0)
        w4_sc = tile([P, 2, H], U8, "w4_sc")
        nc.vector.memset(w4_sc[:].bitcast(I32), 0)
        v_sc = [tile([P, S], U8, f"v_sc{a}") for a in range(2)]
        nc.vector.memset(v_sc[1][:].bitcast(I32), 0)
        ident = tile([P, P], F32, "ident")
        make_identity(nc, ident[:])

        def load_w4(b, on=None):
            words = tile([P, 2, PASS // 2], I32, f"w4_raw{b}", on)
            cols = slice(PASS // 2 * b, PASS // 2 * (b + 1))
            nc.sync.dma_start(out=words[:], in_=w4_words.bitcast(I32)[:, :, cols].rearrange("a p c -> p a c"))
            return words

        w4_raw = [load_w4(0)]
        for r in range(4):
            nc.sync.dma_start(
                out=tab_sc[r:P:16, :].bitcast(I32), in_=tab_scales[:, r:16:4, :].bitcast(I32).rearrange("a q c -> q a c")
            )
        idx = lists.tile([P, S // 16], U16, name="idx")
        nc.sync.dma_start(idx[:], offs)

        def load_table(a):
            words = tile([P, T], I32, f"tab{a}")
            nc.sync.dma_start(out=words[:], in_=tab_words[a].rearrange("p t i -> p (t i)").bitcast(I32))
            return words

        power_sb = [tile([P, PACK, M], F32, f"power{b}") for b in range(2)]
        tab = [load_table(0)]
        load_rows(power_sb[0][:, 0:1, :], power, 0, 0, 1)
        for q in range(4):
            nc.sync.dma_start(
                out=w4_sc[32 * q : 32 * q + 4, :, :].bitcast(I32),
                in_=w4_scales[:, 4 * q : 4 * q + 4, :].bitcast(I32).rearrange("a r c -> r a c"),
            )
        load_rows(power_sb[1][:, 0:1, :], power, 1, 0, 1)
        tab.append(load_table(1))
        load_rows(power_sb[1][:, 1:2, :], power, 1, 1, 2)
        nc.vector.tensor_copy(v_sc[0][:], tab_sc[:].indirect(idx[:]))
        nc.sync.dma_start(out=v_sc[1][0:112, :].bitcast(I32), in_=v_sc[0][16:128, :].bitcast(I32))
        w4_raw.append(load_w4(1, "tab_sc"))

        cor_raw = {}

        def load_cor(b, g):
            cor_raw[b, g] = tile([P, PACK, PASS], F32, f"cor{b}{g}")
            load_rows(cor_raw[b, g][:], cor[:, PASS * g : PASS * (g + 1)], b, 0, PACK)

        idx2 = lists.tile([P, M // 16], U16, name="idx2")
        nc.sync.dma_start(idx2[:], offs2)
        wgt_sb = tile([P, M], F32, "wgt_sb")
        nc.sync.dma_start(out=wgt_sb[:], in_=wgt)
        load_rows(power_sb[0][:, 1:PACK, :], power, 0, 1, PACK)
        mic0 = tile([P, PACK, M], F32, "mic0")
        load_rows(mic0[:], mic, 0, 0, PACK)
        mic1_late = tile([P, 2, M], F32, "mic1_late")
        load_rows(mic1_late[:], mic, 1, 2, PACK)
        res1 = tile([P, PACK, M], F32, "res1")
        load_rows(res1[:, 2:PACK, :], mic, 1, 0, 2)
        load_rows(power_sb[1][:, 2:PACK, :], power, 1, 2, PACK)
        load_cor(1, 0)
        load_cor(0, 0)
        load_cor(0, 1)
        load_cor(1, 1)
        gain_sb = tile([P, 2, PACK], F32, "gain_sb")
        nc.sync.dma_start(out=gain_sb[:], in_=gain.rearrange("(g p t) -> p g t", g=2, t=PACK))
        prev_sb = [tile([P, PACK, M], F32, f"prev{g}") for g in range(2)]
        for g, cuts in enumerate(((0, 2, 4), (0, 2, 3, 4))):
            for first, last in zip(cuts, cuts[1:]):
                load_rows(prev_sb[g][:, first:last, :], prev, g, first, last)


        def inverse_root(out, in_):
            nc.scalar.activation(out=out, in_=in_, func=ACT.Abs_reciprocal_sqrt)

        def square(out, in_):
            nc.scalar.activation(out=out, in_=in_, func=ACT.Square)

        def deal_words(b, copy):
            words = tile([P, 2, PACK, 2 * P], U8, f"w4_dealt{b}")
            copy(out=words[:].bitcast(U16), in_=w4_raw[b][:].bitcast(U16).rearrange("p a (c i) -> p a i c", i=PACK))
            return words

        def deal_scales(b):
            scales = tile([P, 2, PACK, P], U8, f"w4_sc_dealt{b}")
            raw = w4_sc[:, :, PASS * b : PASS * (b + 1)]
            nc.vector.tensor_copy(out=scales[:], in_=raw.rearrange("p a (c i) -> p a i c", i=PACK))
            return scales

        w4_dealt = [deal_words(0, nc.vector.tensor_copy)]

        v = [tile([P, S], U32, f"v{a}") for a in range(2)]
        nc.vector.tensor_copy(v[0][:], tab[0][:].bitcast(U32).indirect(idx[:]))
        w4_sc_dealt = [deal_scales(b) for b in range(2)]
        quarters = (slice(BANK, BANK + BANK // 2), slice(BANK + BANK // 2, S))
        for cols in (slice(0, BANK),) + quarters:
            nc.vector.tensor_copy(
                v[1][:, cols], tab[1][:].bitcast(U32).indirect(idx[:, cols.start // 16 : cols.stop // 16])
            )
        w4_dealt.append(deal_words(1, nc.vector.tensor_copy))

        def block(rows, i, blk):
            return rows[:, i, P * blk : P * (blk + 1)]

        def turned_cols(i):
            place = 2 * (i % 2) + i // 2
            return slice(P * place, P * (place + 1))

        inverse0 = tile([P, BLOCKS, BANK], F32, "inverse0")

        def turn_power(i, number):
            acc = bank(number)
            for blk in range(BLOCKS):
                nc.tensor.transpose(acc[:, P * blk : P * (blk + 1)], block(power_sb[0], i, blk), ident[:])
            return acc

        roots0 = tile([P, BLOCKS, BANK], F32, "roots0")

        def turned_root(i, acc):
            inverse_root(roots0[:, :, turned_cols(i)], acc[:].rearrange("p (k c) -> p k c", k=BLOCKS))

        turned_root(0, turn_power(0, H_BANKS))
        square(inverse0[:, :, 0:P], roots0[:, :, 0:P])
        for i in range(2):
            root_early = tile([P, M], F32, f"root_early{i}")
            inverse_root(root_early[:], power_sb[1][:, i, :])
            square(power_sb[1][:, i, :], root_early[:])

        cor_bf = {}
        cor_mx = {}

        def quantize(values, name, on=None):
            codes = tile([P, BANK], U32, f"{name}_codes", on)
            scales = tile([P, BANK], U8, f"{name}_sc")
            nc.vector.quantize_mx(out=codes[:].bitcast(FP8X4), scales=scales[:], in_=values)
            return codes, scales

        def round_cor(b, g, engine, on=None, cols=slice(0, P)):
            if (b, g) not in cor_bf:
                cor_bf[b, g] = tile([P, PACK, P, PACK], BF16, f"cor_bf{b}{g}", on)
            dealt = cor_bf[b, g][:, :, cols, :]
            raw = cor_raw[b, g][:].rearrange("p j (c t) -> p j c t", t=PACK)[:, :, cols, :]
            if engine == "vector":
                nc.vector.tensor_copy(
                    out=dealt.rearrange("p (u e) c j -> p u c j e", e=2),
                    in_=raw.rearrange("p j c (u e) -> p u c j e", e=2),
                )
            else:
                nc.scalar.copy(out=dealt.rearrange("p t c j -> p c j t"), in_=raw.rearrange("p j c t -> p c j t"))

        def quantize_cor(b, g, on=None):
            cor_mx[b, g] = quantize(cor_bf[b, g][:].rearrange("p t c j -> p (t c j)"), f"cor{b}{g}", on)

        h = {}
        h_acc = {}

        def half_cols(half):
            return slice(BANK * half, BANK * (half + 1))

        def filter_pass(a, b, i, cols, number=None):
            if a == 0:
                if number is None:
                    number = (2 * (PACK * b + i) + cols.start // BANK) % H_BANKS
                h_acc[b, i, cols.start] = bank(number)[:, 0 : cols.stop - cols.start]
            nc.tensor.matmul_mx(
                out=h_acc[b, i, cols.start],
                lhsT=w4_dealt[b][:, a, i, :].bitcast(FP4X4),
                lhsT_scale=w4_sc_dealt[b][:, a, i, :],
                rhs=v[a][:, cols].bitcast(FP8X4),
                rhs_scale=v_sc[a][:, cols],
                start=(a == 0),
                stop=(a == 1),
            )

        def finish(b, i, cols):
            filter_pass(1, b, i, cols)
            if cols.start == 0:
                h[b, i] = tile([P, S], F32, f"h{b}{i}", "root_early1" if (b, i) == (0, 0) else None)
            nc.scalar.activation(
                out=h[b, i][:, cols],
                in_=h_acc[b, i, cols.start],
                func=ACT.Copy,
                scale=(-1.0, 1.0)[b],
            )

        def filter_rows(b, i):
            for half in range(2):
                filter_pass(0, b, i, half_cols(half))
                finish(b, i, half_cols(half))

        x = [tile([P, PACK, M], F32, f"x{b}", ("tab0", None)[b]) for b in range(2)]

        def pick(b, i):
            nc.vector.tensor_tensor(x[b][:, i, :], h[b, i][:].indirect(idx2[:]), wgt_sb[:], ALU.mult)

        filter_pass(0, 0, 0, half_cols(0))
        filter_pass(0, 0, 0, quarters[0])
        filter_pass(0, 0, 0, quarters[1], H_BANKS + 1)
        finish(0, 0, half_cols(0))
        filter_pass(0, 0, 1, half_cols(0))
        finish(0, 0, quarters[0])
        finish(0, 0, quarters[1])
        finish(0, 1, half_cols(0))
        filter_pass(0, 0, 1, half_cols(1))
        finish(0, 1, half_cols(1))
        filter_rows(0, 2)
        turned_late = [turn_power(1, H_BANKS + 1), turn_power(2, H_BANKS)]
        for b in range(2):
            for i in range(PACK):
                if PACK * b + i >= H_BANKS // 2:
                    filter_rows(b, i)
                pick(b, i)
        turned_late.append(turn_power(3, H_BANKS - 2))

        for i, acc in enumerate(turned_late):
            turned_root(1 + i, acc)
        for blks, cols in ((slice(0, 2), slice(P, 3 * P)), (slice(0, 2), slice(3 * P, BANK)), (slice(2, BLOCKS), slice(P, BANK))):
            square(inverse0[:, blks, cols], roots0[:, blks, cols])
        halves = (slice(0, M // 2), slice(M // 2, M))
        root1 = [tile([P, M], F32, f"root1{i}", on) for i, on in ((2, "h12"), (3, "h11"))]
        for root, i in zip(root1, (2, 3)):
            inverse_root(root[:], power_sb[1][:, i, :])
        for root, i in zip(root1, (2, 3)):
            square(power_sb[1][:, i, :], root[:])

        nc.vector.tensor_tensor(res1[:, 0:2, :], res1[:, 2:PACK, :], x[1][:, 0:2, :], ALU.subtract)
        nc.gpsimd.tensor_tensor(res1[:, 2:PACK, :], mic1_late[:], x[1][:, 2:PACK, :], ALU.subtract)

        z_turned = {}

        def normalize_turned(blk):
            acc = bank((H_BANKS - 1 + blk) % H_BANKS)
            for n, rows in enumerate((mic0, x[0])):
                for i in range(PACK):
                    nc.tensor.matmul(
                        acc[:, turned_cols(i)],
                        block(rows, i, blk),
                        ident[:],
                        start=(n == 0 and i == 0),
                        stop=(n == 1 and i == PACK - 1),
                        is_transpose=True,
                    )
            z_turned[blk] = tile([P, BANK], BF16, f"z_turned{blk}")
            nc.vector.tensor_tensor(
                z_turned[blk][:].rearrange("p (c d e) -> p c e d", d=2, e=2),
                acc[:].rearrange("p (e c d) -> p c e d", e=2, d=2),
                inverse0[:, blk, :].rearrange("p (e c d) -> p c e d", e=2, d=2),
                ALU.mult,
            )

        for blk in range(BLOCKS):
            normalize_turned(blk)

        z0 = tile([P, M, PACK], BF16, "z0", "v0")

        def turn_back(half):
            acc = bank(H_BANKS + half)
            for j in range(2):
                words = z_turned[2 * half + j][:].bitcast(F32)
                for u in range(2):
                    at = 2 * P * u + P * j
                    nc.tensor.transpose(acc[:, at : at + P], words[:, P * u : P * (u + 1)], ident[:])
            nc.scalar.copy(
                out=z0[:, 2 * P * half : 2 * P * (half + 1), :].bitcast(F32).rearrange("p (c d) u -> p c u d", d=2),
                in_=acc[:].rearrange("p (u c d) -> p c u d", u=2, d=2),
            )

        def by_runs(rows):
            return rows.rearrange("p i (c e) -> p c i e", e=RUN)

        def words_by_runs(words):
            return words.rearrange("p (c e) i -> p c i e", e=RUN)

        z1 = tile([P, M, PACK], BF16, "z1")

        def quantize_z(b, z, on):
            return quantize(z[:].rearrange("p m i -> p (m i)"), f"z{b}", on)

        round_cor(1, 0, "scalar", "h12", slice(VECTOR_COR, P))
        turn_back(0)
        turn_back(1)
        round_cor(0, 1, "scalar", "z_turned3")
        round_cor(1, 0, "vector", None, slice(0, VECTOR_COR))
        nc.vector.tensor_tensor(words_by_runs(z1[:]), by_runs(res1[:]), by_runs(power_sb[1][:]), ALU.mult)
        quantize_cor(1, 0, "h01")
        z_mx = {1: quantize_z(1, z1, "h11")}
        round_cor(0, 0, "vector", "res1")
        z_mx[0] = quantize_z(0, z0, "h03")
        quantize_cor(0, 0, "h02")
        round_cor(1, 1, "scalar")
        quantize_cor(0, 1, "h10")
        quantize_cor(1, 1, "h13")

        scaled = {}
        for t in range(PACK):
            row = tile([P, M], F32, f"scaled{t}")
            scaled[0, t] = row[:]
            nc.scalar.activation(out=row[:], in_=prev_sb[0][:, t, :], func=ACT.Copy, scale=gain_sb[:, 0, t : t + 1])
        late = tile([P, PACK, M], F32, "scaled_late", "cor_bf11")
        for t in range(PACK):
            scaled[1, t] = late[:, t, :]
            nc.gpsimd.tensor_scalar(scaled[1, t], prev_sb[1][:, t, :], gain_sb[:, 1, t : t + 1], 0.0, ALU.mult, ALU.add)
        y = [tile([P, PACK, M], F32, f"y{g}", f"power{g}") for g in range(2)]

        def product(acc, b, g, t):
            cols = slice(P * t, P * (t + 1))
            nc.tensor.matmul_mx(
                out=acc[:],
                lhsT=cor_mx[b, g][0][:, cols].bitcast(FP8X4),
                lhsT_scale=cor_mx[b, g][1][:, cols],
                rhs=z_mx[b][0][:].bitcast(FP8X4),
                rhs_scale=z_mx[b][1][:],
                start=(b != g),
                stop=(b == g),
            )

        for g in range(2):
            accs = [bank(number) for number in ((3, 4, 5, 0), (1, 2, 6, 7))[g]]
            for t in range(PACK):
                product(accs[t], 1 - g, g, t)
            for t in range(PACK):
                product(accs[t], g, g, t)
                nc.vector.scalar_tensor_tensor(
                    y[g][:, t, :], accs[t][:], gain_sb[:, g, t : t + 1], scaled[g, t], ALU.mult, ALU.add
                )
                if t % 2:
                    nc.sync.dma_start(out=group_rows(out_0, g)[:, t - 1 : t + 1, :], in_=y[g][:, t - 1 : t + 1, :])

        y_sc = tile([P, 2, M], U8, "y_sc")

        def round_y(copy, g, cols, on):
            rounded = tile([P, cols.stop - cols.start, PACK], BF16, f"y_bf{g}{cols.start}", on)
            copy(out=words_by_runs(rounded[:]), in_=by_runs(y[g][:, :, cols]))
            return g, cols, rounded

        pieces = [
            round_y(nc.scalar.copy, 0, slice(0, M), "root_early1"),
            round_y(nc.vector.tensor_copy, 1, halves[1], "h01"),
            round_y(nc.scalar.copy, 1, halves[0], None),
        ]
        for g, cols, rounded in pieces:
            codes = tile([P, cols.stop - cols.start], I32, f"y_codes{g}{cols.start}")
            nc.vector.quantize_mx(
                out=codes[:].bitcast(FP8X4), scales=y_sc[:, g, cols], in_=rounded[:].rearrange("p m t -> p (m t)")
            )
            nc.sync.dma_start(out=out_1[g].rearrange("p m t -> p (m t)").bitcast(I32)[:, cols], in_=codes[:])
        for q in range(4):
            queue = nc.scalar if q % 2 else nc.sync
            queue.dma_start(
                out=out_2[:, 4 * q : 4 * q + 4, :].bitcast(I32).rearrange("g r m -> r g m"),
                in_=y_sc[32 * q : 32 * q + 4, :, :].bitcast(I32),
            )
